import numpy as np
import ml_dtypes


def mxq(x, axis, fmt="e4m3"):
    dtype, down = {"e4m3": (ml_dtypes.float8_e4m3fn, 7), "e5m2": (ml_dtypes.float8_e5m2, 14)}[fmt]
    v = np.moveaxis(np.asarray(x, np.float32).astype(ml_dtypes.bfloat16).astype(np.float64), axis, -1)
    blocks = v.reshape(v.shape[:-1] + (-1, 32))
    amax = np.abs(blocks).max(-1, keepdims=True)
    byte = np.maximum(np.where(amax > 0, np.frexp(amax)[1] - 1 + 127, 0) - down, 1)
    scale = np.exp2(byte - 127.0)
    codes = (blocks / scale).astype(np.float32).astype(dtype).astype(np.float64)
    return np.moveaxis((codes * scale).reshape(v.shape), -1, axis)


WIDE = False


def mx_kscale(k):
    if not WIDE:
        return np.ones(k)
    levels = np.array([10, -10, 5, -5, 0])
    if k % 512:
        return np.exp2(np.random.permutation(np.resize(levels, k // 32))).repeat(32)
    a = np.empty((k // 512, 16))
    for p in range(k // 512):
        a[p, :8] = np.random.permutation(np.resize(levels, 8))
        for g in range(8):
            far = levels[np.abs(levels - a[p, g]) >= 10]
            a[p, g + 8] = far[np.random.randint(len(far))]
    return np.exp2(a.ravel()).repeat(32)


def f64(x):
    return np.asarray(x).astype(np.float64)


def striped(idx):
    return np.tile(idx.reshape(-1, 16).T, (8, 1)).astype(np.uint16)


def unstriped(offs):
    return offs[:16].T.reshape(-1).astype(np.int64)


def sigmoid(v):
    return 1.0 / (1.0 + np.exp(-np.maximum(v, -700.0)))


K, T, E, C, H, N = 1024, 512, 6, 256, 512, 128
TOP = 3


def by_expert(wq, xq):
    return np.concatenate([wq[e].T @ xq[:, e * C:(e + 1) * C] for e in range(E)], axis=1)


def setup_inputs():
    n = np.random.standard_normal
    s = mx_kscale(K)[:, None]
    u = mx_kscale(H)
    deal = np.repeat(np.arange(E), C).reshape(TOP, T)[:, np.random.permutation(T)]
    deal = np.take_along_axis(deal, np.argsort(np.random.rand(TOP, T), axis=0), axis=0)
    for _ in range(8):
        s_, t_ = np.random.permutation(T).reshape(2, -1); r = np.random.randint(TOP, size=T // 2); x, y = deal[r, s_].copy(), deal[r, t_].copy()
        ok = ~((deal[:, s_] == y).any(0) | (deal[:, t_] == x).any(0)); deal[r[ok], s_[ok]] = y[ok]; deal[r[ok], t_[ok]] = x[ok]
    order = np.lexsort((np.random.rand(TOP * T), deal.reshape(-1)))
    slot_token = order % T; pos = np.empty(TOP * T, np.int64); pos[order] = np.arange(TOP * T); pos = pos.reshape(TOP, T)
    g = np.random.uniform(0.5, 1.5, (TOP, T)); g = g / g.sum(0)
    return {
        "xT": (n((K, T)) * s).astype(np.float32),
        "w1": (n((E, K, H)) / np.sqrt(K) / s[None]).astype(np.float32),
        "w3": (n((E, K, H)) / np.sqrt(K) / s[None] * u[None, None, :]).astype(np.float32),
        "w2": (n((E, H, N)) / np.sqrt(H) / u[None, :, None]).astype(np.float32),
        "gate": np.stack([np.tile(r, (N, 1)) for r in g]).astype(np.float32),
        "offs": striped(slot_token),
        "pos1": striped(pos[0]),
        "pos2": striped(pos[1]),
        "pos3": striped(pos[2]),
    }


def reference(xT, w1, w3, w2, gate, offs, pos1, pos2, pos3):
    idx = unstriped(offs)
    xq = mxq(f64(xT)[:, idx], 0, "e4m3")
    h = sigmoid(by_expert(mxq(f64(w1), 1, "e4m3"), xq))
    h = h * by_expert(mxq(f64(w3), 1, "e4m3"), xq)
    y = by_expert(mxq(f64(w2), 1, "e4m3"), mxq(h, 0, "e4m3"))
    return sum(f64(gate[r]) * y[:, unstriped(p)] for r, p in enumerate((pos1, pos2, pos3)))

@@ -1,0 +1,198 @@
+from contextlib import ExitStack
+
+import concourse.mybir as mybir
+
+K, T, E, C, H, N = 1024, 512, 6, 256, 512, 128
+TOP = 3
+FLOPS = 2 * E * C * (2 * K * H + H * N)
+
+F32 = mybir.dt.float32
+BF16 = mybir.dt.bfloat16
+U32 = mybir.dt.uint32
+U16 = mybir.dt.uint16
+U8 = mybir.dt.uint8
+FP8X4 = mybir.dt.float8_e4m3fn_x4
+MULT = mybir.AluOpType.mult
+ADD = mybir.AluOpType.add
+SIGMOID = mybir.ActivationFunctionType.Sigmoid
+
+P = 128
+PACK = 4
+K_PASS = P * PACK
+PASSES = K // K_PASS
+HALF = C // 2
+PLANE = 4
+SCALAR_SHARE = 80
+SCALAR_SHARE_LAST = 44
+COMBINE = (256, 256)
+
+
+def tile_moe_tk_glu_sigmoid_kernel(tc, xT, w1, w3, w2, gate, offs, pos1, pos2, pos3, out):
+    nc = tc.nc
+
+    with ExitStack() as ctx:
+        held = ctx.enter_context(tc.tile_pool(name="held", bufs=1))
+        loads = ctx.enter_context(tc.tile_pool(name="loads", bufs=14))
+        work = ctx.enter_context(tc.tile_pool(name="work", bufs=4))
+        quant = ctx.enter_context(tc.tile_pool(name="quant", bufs=8))
+        gathered = ctx.enter_context(tc.tile_pool(name="gathered", bufs=2))
+        psum = ctx.enter_context(tc.psum_pool(name="psum", bufs=3))
+        psum_y = ctx.enter_context(tc.psum_pool(name="psum_y", bufs=2))
+
+        def load_rows(rows):
+            raw = loads.tile([P, PACK, rows.shape[1]], F32, name="raw", tag="raw")
+            nc.sync.dma_start(out=raw[:], in_=rows.rearrange("(p j) w -> p j w", j=PACK))
+            return raw
+
+        def quantize(codes, scales, grouped):
+            nc.vector.quantize_mx(out=codes.bitcast(FP8X4), scales=scales, in_=grouped)
+
+        def interleave(copy, grouped, raw, c0, c1):
+            copy(
+                out=grouped[:, c0:c1, :].rearrange("p (c i) j -> p c j i", i=4),
+                in_=raw[:, :, c0:c1].rearrange("p j (c i) -> p c j i", i=4),
+            )
+
+        def interleave_permuted(copy, grouped, raw, m0, m1):
+            copy(
+                out=grouped[:, :, m0:m1, :].rearrange("p t m j -> p m j t"),
+                in_=raw[:, :, PACK * m0 : PACK * m1].rearrange("p j (m t) -> p m j t", t=PACK),
+            )
+
+        warm = held.tile([P, 8], F32, name="warm")
+        warm_out = held.tile([P, 8], F32, name="warm_out")
+        nc.vector.memset(warm[:], 0.0)
+        nc.scalar.activation(out=warm_out[:], in_=warm[:], func=SIGMOID)
+
+        x_raw = [load_rows(xT[s * K_PASS : (s + 1) * K_PASS, :]) for s in range(PASSES)]
+        slot_token = held.tile([P, E * C // 16], U16, name="slot_token")
+        nc.sync.dma_start(slot_token[:], offs)
+
+        x_codes = []
+        x_scales = held.tile([P, T], U8, name="x_scales", align_bytes=64)
+        nc.gpsimd.memset(x_scales[:], 0)
+        for s in range(PASSES):
+            codes = held.tile([P, T], U32, name="x_codes%d" % s, align_bytes=64)
+            x_grouped = work.tile([P, T, PACK], BF16, name="x_grouped", tag="grouped", align_bytes=64)
+            interleave(nc.scalar.copy, x_grouped, x_raw[s], 0, 176)
+            interleave(nc.vector.tensor_copy, x_grouped, x_raw[s], 176, T)
+            quantize(codes[:], x_scales[PLANE * s :, :], x_grouped[:].rearrange("p c j -> p (c j)"))
+            x_codes.append(codes)
+
+        y = held.tile([P, E * C], F32, name="y")
+
+        def quantized_first_layer(w, e, s, last):
+            raw = load_rows(w[e, s * K_PASS : (s + 1) * K_PASS, :])
+            grouped = work.tile([P, PACK, P, PACK], BF16, name="w_grouped", tag="grouped", align_bytes=64)
+            share = SCALAR_SHARE_LAST if last else SCALAR_SHARE
+            interleave_permuted(nc.scalar.copy, grouped, raw, 0, share)
+            interleave_permuted(nc.vector.tensor_copy, grouped, raw, share, P)
+            codes = quant.tile([P, H], U32, name="w_codes", align_bytes=64)
+            scales = quant.tile([P, H], U8, name="w_scales", align_bytes=64)
+            if last:
+                for t in range(PACK):
+                    cols = slice(t * P, (t + 1) * P)
+                    quantize(codes[:, cols], scales[:, cols], grouped[:, t, :, :].rearrange("p m j -> p (m j)"))
+            else:
+                quantize(codes[:], scales[:], grouped[:].rearrange("p t m j -> p (t m j)"))
+            return codes, scales, raw
+
+        def second_layer(acc, e, c0, c1, w2_q, h_q):
+            nc.tensor.matmul_mx(
+                out=acc,
+                lhsT=w2_q[0][:].bitcast(FP8X4),
+                lhsT_scale=w2_q[1][:],
+                rhs=h_q[0][:, c0:c1].bitcast(FP8X4),
+                rhs_scale=h_q[1][:, c0:c1],
+                start=True,
+                stop=True,
+            )
+            nc.scalar.copy(out=y[:, e * C + c0 : e * C + c1], in_=acc)
+
+        def first_layer(acc, weights, slot_codes, slot_scales, slots):
+            for t in range(PACK):
+                cols = slice(t * P, (t + 1) * P)
+                for s in range(PASSES):
+                    nc.tensor.matmul_mx(
+                        out=acc[:, t, :],
+                        lhsT=weights[s][0][:, cols].bitcast(FP8X4),
+                        lhsT_scale=weights[s][1][:, cols],
+                        rhs=slot_codes[:, s, slots].bitcast(FP8X4),
+                        rhs_scale=slot_scales[PLANE * s :, slots],
+                        start=(s == 0),
+                        stop=(s == PASSES - 1),
+                    )
+
+        pending = None
+        for e in range(E):
+            slot_codes = gathered.tile([P, PASSES, C], U32, name="slot_codes", align_bytes=64)
+            slot_scales = gathered.tile([P, C], U8, name="slot_scales", align_bytes=64)
+            picks = slot_token[:, e * C // 16 : (e + 1) * C // 16]
+            for s in range(PASSES):
+                nc.vector.tensor_copy(slot_codes[:, s, :], x_codes[s][:].indirect(picks))
+            nc.vector.tensor_copy(slot_scales[:], x_scales[:].indirect(picks))
+
+            halves = [slice(u * HALF, (u + 1) * HALF) for u in range(2)]
+            w1_q = [quantized_first_layer(w1, e, s, False) for s in range(PASSES)]
+            a = []
+            for u in range(2):
+                a_u = psum.tile([P, PACK, HALF], F32, name="a")
+                first_layer(a_u, w1_q, slot_codes, slot_scales, halves[u])
+                a.append(a_u)
+
+            w3_q = [quantized_first_layer(w3, e, s, e == E - 1 and s == PASSES - 1) for s in range(PASSES)]
+            spent = w3_q[PASSES - 1][2]
+            sig = []
+            for u in range(2):
+                sig_u = spent[:, 2 * u : 2 * u + 2, 0 : 2 * HALF].rearrange("p g (c t) -> p g c t", t=PACK)
+                nc.scalar.activation(out=sig_u, in_=a[u][:].rearrange("p t (g c) -> p g c t", g=2), func=SIGMOID)
+                sig.append(sig_u)
+            if pending is not None:
+                second_layer(a[0][:, 0:2, :].rearrange("p t c -> p (t c)"), e - 1, 0, C, *pending)
+
+            w2_raw = load_rows(w2[e])
+            w2_grouped = work.tile([P, N, PACK], BF16, name="w2_grouped", align_bytes=64)
+            interleave(nc.scalar.copy, w2_grouped, w2_raw, 0, N)
+            w2_codes = work.tile([P, N], U32, name="w2_codes", align_bytes=64)
+            w2_scales = work.tile([P, N], U8, name="w2_scales", align_bytes=64)
+            quantize(w2_codes[:], w2_scales[:], w2_grouped[:].rearrange("p c j -> p (c j)"))
+
+            h_codes = work.tile([P, C], U32, name="h_codes", align_bytes=64)
+            h_scales = work.tile([P, C], U8, name="h_scales", align_bytes=64)
+            pending = ((w2_codes, w2_scales), (h_codes, h_scales))
+            for u in range(2):
+                b = psum.tile([P, PACK, HALF], F32, name="b")
+                first_layer(b, w3_q, slot_codes, slot_scales, halves[u])
+                h = work.tile([P, HALF, PACK], BF16, name="h", align_bytes=64)
+                nc.vector.tensor_tensor(
+                    h[:].rearrange("p (g c) t -> p g c t", g=2),
+                    b[:].rearrange("p t (g c) -> p g c t", g=2),
+                    sig[u],
+                    MULT,
+                )
+                quantize(h_codes[:, halves[u]], h_scales[:, halves[u]], h[:].rearrange("p c t -> p (c t)"))
+                if e == E - 1:
+                    y_acc = psum_y.tile([P, HALF], F32, name="y_acc")
+                    second_layer(y_acc[:], e, u * HALF, (u + 1) * HALF, *pending)
+
+        gates = loads.tile([P, TOP, T], F32, name="gates", tag="raw")
+        nc.sync.dma_start(out=gates[:], in_=gate.rearrange("r n t -> n r t"))
+        token_slot = []
+        for r, pos in enumerate((pos1, pos2, pos3)):
+            tile = held.tile([P, T // 16], U16, name="token_slot%d" % r)
+            nc.sync.dma_start(tile[:], pos)
+            token_slot.append(tile)
+
+        products = held.tile([P, TOP, T], F32, name="products")
+        partial = held.tile([P, T], F32, name="partial")
+        total = held.tile([P, T], F32, name="total")
+        t0 = 0
+        for width in COMBINE:
+            tokens = slice(t0, t0 + width)
+            for r in range(TOP):
+                picks = token_slot[r][:, t0 // 16 : (t0 + width) // 16]
+                nc.vector.tensor_tensor(products[:, r, tokens], y[:].indirect(picks), gates[:, r, tokens], MULT)
+            nc.vector.tensor_tensor(partial[:, tokens], products[:, 0, tokens], products[:, 1, tokens], ADD)
+            nc.vector.tensor_tensor(total[:, tokens], partial[:, tokens], products[:, 2, tokens], ADD)
+            nc.sync.dma_start(out=out[:, tokens], in_=total[:, tokens])
+            t0 += width

@@ -22,21 +22,26 @@ K_PASS = P * PACK
 PASSES = K // K_PASS
 HALF = C // 2
 PLANE = 4
-SCALAR_SHARE = 80
-SCALAR_SHARE_LAST = 44
+TURNS = 3
+X_SCALAR_COLUMNS = 176
+SCALAR_SHARE = (80, 96, 64, 96)
+SCALAR_SHARE_LAST = (64, 80, 72, 52)
+W2_CAST = (("scalar", "vector"), ("vector", "vector"), ("scalar", "scalar"))
 COMBINE = (256, 256)
 
 
 def tile_moe_tk_glu_sigmoid_kernel(tc, xT, w1, w3, w2, gate, offs, pos1, pos2, pos3, out):
     nc = tc.nc
+    copy_on = {"scalar": nc.scalar.copy, "vector": nc.vector.tensor_copy}
 
     with ExitStack() as ctx:
         held = ctx.enter_context(tc.tile_pool(name="held", bufs=1))
+        turns = ctx.enter_context(tc.tile_pool(name="turns", bufs=1))
         loads = ctx.enter_context(tc.tile_pool(name="loads", bufs=14))
         work = ctx.enter_context(tc.tile_pool(name="work", bufs=4))
         quant = ctx.enter_context(tc.tile_pool(name="quant", bufs=8))
-        gathered = ctx.enter_context(tc.tile_pool(name="gathered", bufs=2))
-        psum = ctx.enter_context(tc.psum_pool(name="psum", bufs=3))
+        psum_a = ctx.enter_context(tc.psum_pool(name="psum_a", bufs=2))
+        psum_b = ctx.enter_context(tc.psum_pool(name="psum_b", bufs=2))
         psum_y = ctx.enter_context(tc.psum_pool(name="psum_y", bufs=2))
 
         def load_rows(rows):
@@ -47,10 +52,10 @@ def tile_moe_tk_glu_sigmoid_kernel(tc, xT, w1, w3, w2, gate, offs, pos1, pos2, p
         def quantize(codes, scales, grouped):
             nc.vector.quantize_mx(out=codes.bitcast(FP8X4), scales=scales, in_=grouped)
 
-        def interleave(copy, grouped, raw, c0, c1):
+        def interleave(copy, grouped, raw):
             copy(
-                out=grouped[:, c0:c1, :].rearrange("p (c i) j -> p c j i", i=4),
-                in_=raw[:, :, c0:c1].rearrange("p j (c i) -> p c j i", i=4),
+                out=grouped.rearrange("p (c i) j -> p c j i", i=4),
+                in_=raw.rearrange("p j (c i) -> p c j i", i=4),
             )
 
         def interleave_permuted(copy, grouped, raw, m0, m1):
@@ -74,42 +79,45 @@ def tile_moe_tk_glu_sigmoid_kernel(tc, xT, w1, w3, w2, gate, offs, pos1, pos2, p
         for s in range(PASSES):
             codes = held.tile([P, T], U32, name="x_codes%d" % s, align_bytes=64)
             x_grouped = work.tile([P, T, PACK], BF16, name="x_grouped", tag="grouped", align_bytes=64)
-            interleave(nc.scalar.copy, x_grouped, x_raw[s], 0, 176)
-            interleave(nc.vector.tensor_copy, x_grouped, x_raw[s], 176, T)
+            for copy, cols in ((nc.scalar.copy, slice(0, X_SCALAR_COLUMNS)), (nc.vector.tensor_copy, slice(X_SCALAR_COLUMNS, T))):
+                interleave(copy, x_grouped[:, cols, :], x_raw[s][:, :, cols])
             quantize(codes[:], x_scales[PLANE * s :, :], x_grouped[:].rearrange("p c j -> p (c j)"))
             x_codes.append(codes)
 
         y = held.tile([P, E * C], F32, name="y")
+        h_codes = held.tile([P, E * C], U32, name="h_codes", align_bytes=64)
+        h_scales = held.tile([P, E * C], U8, name="h_scales", align_bytes=64)
+        w2_codes = held.tile([P, E * N], U32, name="w2_codes", align_bytes=64)
+        w2_scales = held.tile([P, E * N], U8, name="w2_scales", align_bytes=64)
+        slot_codes, slot_scales = {}, {}
 
-        def quantized_first_layer(w, e, s, last):
+        def picks(e):
+            return slot_token[:, e * C // 16 : (e + 1) * C // 16]
+
+        def gather_codes(e):
+            slot_codes[e] = turns.tile([P, PASSES, C], U32, name="slot_codes", tag="codes_turn%d" % (e % TURNS), align_bytes=64)
+            for s in range(PASSES):
+                nc.vector.tensor_copy(slot_codes[e][:, s, :], x_codes[s][:].indirect(picks(e)))
+
+        def gather_scales(e):
+            slot_scales[e] = turns.tile([P, C], U8, name="slot_scales", tag="scales_turn%d" % (e % TURNS), align_bytes=64)
+            nc.vector.tensor_copy(slot_scales[e][:], x_scales[:].indirect(picks(e)))
+
+        def quantized_weights(w, e, s, share, pool, tag, pieces):
             raw = load_rows(w[e, s * K_PASS : (s + 1) * K_PASS, :])
-            grouped = work.tile([P, PACK, P, PACK], BF16, name="w_grouped", tag="grouped", align_bytes=64)
-            share = SCALAR_SHARE_LAST if last else SCALAR_SHARE
+            grouped = pool.tile([P, PACK, P, PACK], BF16, name="w_grouped", tag=tag, align_bytes=64)
             interleave_permuted(nc.scalar.copy, grouped, raw, 0, share)
             interleave_permuted(nc.vector.tensor_copy, grouped, raw, share, P)
             codes = quant.tile([P, H], U32, name="w_codes", align_bytes=64)
             scales = quant.tile([P, H], U8, name="w_scales", align_bytes=64)
-            if last:
-                for t in range(PACK):
-                    cols = slice(t * P, (t + 1) * P)
-                    quantize(codes[:, cols], scales[:, cols], grouped[:, t, :, :].rearrange("p m j -> p (m j)"))
-            else:
-                quantize(codes[:], scales[:], grouped[:].rearrange("p t m j -> p (t m j)"))
+            step = PACK // pieces
+            for t in range(0, PACK, step):
+                cols = slice(t * P, (t + step) * P)
+                quantize(codes[:, cols], scales[:, cols], grouped[:, t : t + step, :, :].rearrange("p t m j -> p (t m j)"))
             return codes, scales, raw
 
-        def second_layer(acc, e, c0, c1, w2_q, h_q):
-            nc.tensor.matmul_mx(
-                out=acc,
-                lhsT=w2_q[0][:].bitcast(FP8X4),
-                lhsT_scale=w2_q[1][:],
-                rhs=h_q[0][:, c0:c1].bitcast(FP8X4),
-                rhs_scale=h_q[1][:, c0:c1],
-                start=True,
-                stop=True,
-            )
-            nc.scalar.copy(out=y[:, e * C + c0 : e * C + c1], in_=acc)
-
-        def first_layer(acc, weights, slot_codes, slot_scales, slots):
+        def first_layer(acc, weights, e, u):
+            slots = slice(u * HALF, (u + 1) * HALF)
             for t in range(PACK):
                 cols = slice(t * P, (t + 1) * P)
                 for s in range(PASSES):
@@ -117,71 +125,101 @@ def tile_moe_tk_glu_sigmoid_kernel(tc, xT, w1, w3, w2, gate, offs, pos1, pos2, p
                         out=acc[:, t, :],
                         lhsT=weights[s][0][:, cols].bitcast(FP8X4),
                         lhsT_scale=weights[s][1][:, cols],
-                        rhs=slot_codes[:, s, slots].bitcast(FP8X4),
-                        rhs_scale=slot_scales[PLANE * s :, slots],
+                        rhs=slot_codes[e][:, s, slots].bitcast(FP8X4),
+                        rhs_scale=slot_scales[e][PLANE * s :, slots],
                         start=(s == 0),
                         stop=(s == PASSES - 1),
                     )
 
-        pending = None
-        for e in range(E):
-            slot_codes = gathered.tile([P, PASSES, C], U32, name="slot_codes", align_bytes=64)
-            slot_scales = gathered.tile([P, C], U8, name="slot_scales", align_bytes=64)
-            picks = slot_token[:, e * C // 16 : (e + 1) * C // 16]
-            for s in range(PASSES):
-                nc.vector.tensor_copy(slot_codes[:, s, :], x_codes[s][:].indirect(picks))
-            nc.vector.tensor_copy(slot_scales[:], x_scales[:].indirect(picks))
+        def hidden(h, b, sig, slots):
+            nc.vector.tensor_tensor(
+                h.rearrange("p (g c) t -> p g c t", g=2), b[:].rearrange("p t (g c) -> p g c t", g=2), sig, MULT
+            )
+            quantize(h_codes[:, slots], h_scales[:, slots], h.rearrange("p c t -> p (c t)"))
 
-            halves = [slice(u * HALF, (u + 1) * HALF) for u in range(2)]
-            w1_q = [quantized_first_layer(w1, e, s, False) for s in range(PASSES)]
+        def second_layer(acc, pieces, copy):
+            first, last = pieces[0][1].start, pieces[-1][1].stop
+            for e, slots in pieces:
+                cols = slice(e * N, (e + 1) * N)
+                nc.tensor.matmul_mx(
+                    out=acc[:, slots.start - first : slots.stop - first],
+                    lhsT=w2_codes[:, cols].bitcast(FP8X4),
+                    lhsT_scale=w2_scales[:, cols],
+                    rhs=h_codes[:, slots].bitcast(FP8X4),
+                    rhs_scale=h_scales[:, slots],
+                    start=True,
+                    stop=True,
+                )
+            copy(out=y[:, first:last], in_=acc)
+
+        gather_codes(0)
+        gather_scales(0)
+        gather_codes(1)
+        for e in range(E):
+            last = e == E - 1
+            share = SCALAR_SHARE_LAST if last else SCALAR_SHARE
+            halves = [slice(e * C + u * HALF, e * C + (u + 1) * HALF) for u in range(2)]
+
+            w1_q = [quantized_weights(w1, e, 0, share[0], turns, "scales_turn%d" % ((e + 1) % TURNS), 1)]
+            if not last:
+                gather_scales(e + 1)
+            w1_q.append(quantized_weights(w1, e, 1, share[1], work, "grouped", 1))
             a = []
             for u in range(2):
-                a_u = psum.tile([P, PACK, HALF], F32, name="a")
-                first_layer(a_u, w1_q, slot_codes, slot_scales, halves[u])
+                a_u = psum_a.tile([P, PACK, HALF], F32, name="a")
+                first_layer(a_u, w1_q, e, u)
                 a.append(a_u)
 
-            w3_q = [quantized_first_layer(w3, e, s, e == E - 1 and s == PASSES - 1) for s in range(PASSES)]
+            w3_q = [quantized_weights(w3, e, 0, share[2], work, "grouped", 1)]
+            w3_q.append(quantized_weights(w3, e, 1, share[3], turns, "codes_turn%d" % ((e + 2) % TURNS), 2 if last else 1))
+            if e + 2 < E:
+                gather_codes(e + 2)
+            b = []
+            for u in range(2):
+                b_u = psum_b.tile([P, PACK, HALF], F32, name="b")
+                first_layer(b_u, w3_q, e, u)
+                b.append(b_u)
             spent = w3_q[PASSES - 1][2]
             sig = []
             for u in range(2):
                 sig_u = spent[:, 2 * u : 2 * u + 2, 0 : 2 * HALF].rearrange("p g (c t) -> p g c t", t=PACK)
                 nc.scalar.activation(out=sig_u, in_=a[u][:].rearrange("p t (g c) -> p g c t", g=2), func=SIGMOID)
                 sig.append(sig_u)
-            if pending is not None:
-                second_layer(a[0][:, 0:2, :].rearrange("p t c -> p (t c)"), e - 1, 0, C, *pending)
+            if not last:
+                for u in range(2):
+                    h = work.tile([P, HALF, PACK], BF16, name="h", align_bytes=64)
+                    hidden(h[:], b[u], sig[u], halves[u])
 
-            w2_raw = load_rows(w2[e])
-            w2_grouped = work.tile([P, N, PACK], BF16, name="w2_grouped", align_bytes=64)
-            interleave(nc.scalar.copy, w2_grouped, w2_raw, 0, N)
-            w2_codes = work.tile([P, N], U32, name="w2_codes", align_bytes=64)
-            w2_scales = work.tile([P, N], U8, name="w2_scales", align_bytes=64)
-            quantize(w2_codes[:], w2_scales[:], w2_grouped[:].rearrange("p c j -> p (c j)"))
+        w2_grouped = []
+        for pair in range(E // 2):
+            raw = loads.tile([P, 2, PACK, N], F32, name="w2_raw", tag="raw")
+            nc.sync.dma_start(out=raw[:], in_=w2[2 * pair : 2 * pair + 2].rearrange("e (p j) n -> p e j n", j=PACK))
+            grouped = work.tile([P, 2, N, PACK], BF16, name="w2_grouped", align_bytes=64)
+            for i in range(2):
+                interleave(copy_on[W2_CAST[pair][i]], grouped[:, i, :, :], raw[:, i, :, :])
+            cols = slice(2 * pair * N, (2 * pair + 2) * N)
+            quantize(w2_codes[:, cols], w2_scales[:, cols], grouped[:].rearrange("p e n j -> p (e n j)"))
+            w2_grouped.append(grouped)
+        for u in range(2):
+            hidden(w2_grouped[u][:, 0, :, :], b[u], sig[u], halves[u])
+            y_half = psum_y.tile([P, HALF], F32, name="y_half")
+            second_layer(y_half[:], [(E - 1, halves[u])], nc.vector.tensor_copy)
+        for u in range(2):
+            pieces = [(e, slice(e * C, (e + 1) * C)) for e in (2 * u, 2 * u + 1)]
+            second_layer(b[u][:].rearrange("p t c -> p (t c)"), pieces, nc.scalar.copy)
+        y_whole = psum_y.tile([P, C], F32, name="y_whole")
+        second_layer(y_whole[:], [(E - 2, slice((E - 2) * C, (E - 1) * C))], nc.scalar.copy)
 
-            h_codes = work.tile([P, C], U32, name="h_codes", align_bytes=64)
-            h_scales = work.tile([P, C], U8, name="h_scales", align_bytes=64)
-            pending = ((w2_codes, w2_scales), (h_codes, h_scales))
-            for u in range(2):
-                b = psum.tile([P, PACK, HALF], F32, name="b")
-                first_layer(b, w3_q, slot_codes, slot_scales, halves[u])
-                h = work.tile([P, HALF, PACK], BF16, name="h", align_bytes=64)
-                nc.vector.tensor_tensor(
-                    h[:].rearrange("p (g c) t -> p g c t", g=2),
-                    b[:].rearrange("p t (g c) -> p g c t", g=2),
-                    sig[u],
-                    MULT,
-                )
-                quantize(h_codes[:, halves[u]], h_scales[:, halves[u]], h[:].rearrange("p c t -> p (c t)"))
-                if e == E - 1:
-                    y_acc = psum_y.tile([P, HALF], F32, name="y_acc")
-                    second_layer(y_acc[:], e, u * HALF, (u + 1) * HALF, *pending)
-
-        gates = loads.tile([P, TOP, T], F32, name="gates", tag="raw")
-        nc.sync.dma_start(out=gates[:], in_=gate.rearrange("r n t -> n r t"))
         token_slot = []
         for r, pos in enumerate((pos1, pos2, pos3)):
             tile = held.tile([P, T // 16], U16, name="token_slot%d" % r)
             nc.sync.dma_start(tile[:], pos)
             token_slot.append(tile)
+        gates = []
+        for r in range(TOP):
+            gate_r = loads.tile([P, T], F32, name="gate_r", tag="raw")
+            nc.sync.dma_start(out=gate_r[:], in_=gate[r])
+            gates.append(gate_r)
 
         products = held.tile([P, TOP, T], F32, name="products")
         partial = held.tile([P, T], F32, name="partial")
@@ -190,8 +228,8 @@ def tile_moe_tk_glu_sigmoid_kernel(tc, xT, w1, w3, w2, gate, offs, pos1, pos2, p
         for width in COMBINE:
             tokens = slice(t0, t0 + width)
             for r in range(TOP):
-                picks = token_slot[r][:, t0 // 16 : (t0 + width) // 16]
-                nc.vector.tensor_tensor(products[:, r, tokens], y[:].indirect(picks), gates[:, r, tokens], MULT)
+                slots_of = token_slot[r][:, t0 // 16 : (t0 + width) // 16]
+                nc.vector.tensor_tensor(products[:, r, tokens], y[:].indirect(slots_of), gates[r][:, tokens], MULT)
             nc.vector.tensor_tensor(partial[:, tokens], products[:, 0, tokens], products[:, 1, tokens], ADD)
             nc.vector.tensor_tensor(total[:, tokens], partial[:, tokens], products[:, 2, tokens], ADD)
             nc.sync.dma_start(out=out[:, tokens], in_=total[:, tokens])

@@ -25,9 +25,9 @@ PLANE = 4
 TURNS = 3
 X_SCALAR_COLUMNS = 176
 SCALAR_SHARE = (80, 96, 64, 96)
-SCALAR_SHARE_LAST = (64, 80, 72, 52)
+SCALAR_SHARE_LAST = (64, 80, 72, 64)
 W2_CAST = (("scalar", "vector"), ("vector", "vector"), ("scalar", "scalar"))
-COMBINE = (256, 256)
+COMBINE = (256, 128, 128)
 
 
 def tile_moe_tk_glu_sigmoid_kernel(tc, xT, w1, w3, w2, gate, offs, pos1, pos2, pos3, out):
@@ -201,7 +201,11 @@ def tile_moe_tk_glu_sigmoid_kernel(tc, xT, w1, w3, w2, gate, offs, pos1, pos2, p
             quantize(w2_codes[:, cols], w2_scales[:, cols], grouped[:].rearrange("p e n j -> p (e n j)"))
             w2_grouped.append(grouped)
         for u in range(2):
-            hidden(w2_grouped[u][:, 0, :, :], b[u], sig[u], halves[u])
+            if u == 0:
+                h = w2_grouped[0][:, 0, :, :]
+            else:
+                h = work.tile([P, HALF, PACK], BF16, name="h", align_bytes=64)[:]
+            hidden(h, b[u], sig[u], halves[u])
             y_half = psum_y.tile([P, HALF], F32, name="y_half")
             second_layer(y_half[:], [(E - 1, halves[u])], nc.vector.tensor_copy)
         for u in range(2):
@@ -224,13 +228,23 @@ def tile_moe_tk_glu_sigmoid_kernel(tc, xT, w1, w3, w2, gate, offs, pos1, pos2, p
         products = held.tile([P, TOP, T], F32, name="products")
         partial = held.tile([P, T], F32, name="partial")
         total = held.tile([P, T], F32, name="total")
+        for r in range(TOP - 1):
+            nc.vector.tensor_tensor(products[:, r, :], y[:].indirect(token_slot[r][:]), gates[r][:], MULT)
+
+        def finish(tokens):
+            nc.vector.tensor_tensor(total[:, tokens], partial[:, tokens], products[:, TOP - 1, tokens], ADD)
+            nc.sync.dma_start(out=out[:, tokens], in_=total[:, tokens])
+
         t0 = 0
+        waiting = None
         for width in COMBINE:
             tokens = slice(t0, t0 + width)
-            for r in range(TOP):
-                slots_of = token_slot[r][:, t0 // 16 : (t0 + width) // 16]
-                nc.vector.tensor_tensor(products[:, r, tokens], y[:].indirect(slots_of), gates[r][:, tokens], MULT)
-            nc.vector.tensor_tensor(partial[:, tokens], products[:, 0, tokens], products[:, 1, tokens], ADD)
-            nc.vector.tensor_tensor(total[:, tokens], partial[:, tokens], products[:, 2, tokens], ADD)
-            nc.sync.dma_start(out=out[:, tokens], in_=total[:, tokens])
+            slots_of = token_slot[TOP - 1][:, t0 // 16 : (t0 + width) // 16]
+            nc.vector.tensor_tensor(products[:, TOP - 1, tokens], y[:].indirect(slots_of), gates[TOP - 1][:, tokens], MULT)
+            if waiting is None:
+                nc.vector.tensor_tensor(partial[:], products[:, 0, :], products[:, 1, :], ADD)
+            else:
+                finish(waiting)
+            waiting = tokens
             t0 += width
+        finish(waiting)

@@ -25,14 +25,13 @@ PLANE = 4
 TURNS = 3
 X_SCALAR_COLUMNS = 176
 SCALAR_SHARE = (80, 96, 64, 96)
-SCALAR_SHARE_LAST = (64, 80, 72, 64)
-W2_CAST = (("scalar", "vector"), ("vector", "vector"), ("scalar", "scalar"))
+SCALAR_SHARE_LAST = (64, 64, 48, 44)
+EARLY_W2 = 0
 COMBINE = (256, 128, 128)
 
 
 def tile_moe_tk_glu_sigmoid_kernel(tc, xT, w1, w3, w2, gate, offs, pos1, pos2, pos3, out):
     nc = tc.nc
-    copy_on = {"scalar": nc.scalar.copy, "vector": nc.vector.tensor_copy}
 
     with ExitStack() as ctx:
         held = ctx.enter_context(tc.tile_pool(name="held", bufs=1))
@@ -40,12 +39,13 @@ def tile_moe_tk_glu_sigmoid_kernel(tc, xT, w1, w3, w2, gate, offs, pos1, pos2, p
         loads = ctx.enter_context(tc.tile_pool(name="loads", bufs=14))
         work = ctx.enter_context(tc.tile_pool(name="work", bufs=4))
         quant = ctx.enter_context(tc.tile_pool(name="quant", bufs=8))
+        small = ctx.enter_context(tc.tile_pool(name="small", bufs=E))
         psum_a = ctx.enter_context(tc.psum_pool(name="psum_a", bufs=2))
         psum_b = ctx.enter_context(tc.psum_pool(name="psum_b", bufs=2))
-        psum_y = ctx.enter_context(tc.psum_pool(name="psum_y", bufs=2))
+        psum_y = ctx.enter_context(tc.psum_pool(name="psum_y", bufs=4))
 
         def load_rows(rows):
-            raw = loads.tile([P, PACK, rows.shape[1]], F32, name="raw", tag="raw")
+            raw = loads.tile([P, PACK, rows.shape[1]], F32, name="raw", tag="raw", align_bytes=64)
             nc.sync.dma_start(out=raw[:], in_=rows.rearrange("(p j) w -> p j w", j=PACK))
             return raw
 
@@ -116,19 +116,19 @@ def tile_moe_tk_glu_sigmoid_kernel(tc, xT, w1, w3, w2, gate, offs, pos1, pos2, p
                 quantize(codes[:, cols], scales[:, cols], grouped[:, t : t + step, :, :].rearrange("p t m j -> p (t m j)"))
             return codes, scales, raw
 
-        def first_layer(acc, weights, e, u):
-            slots = slice(u * HALF, (u + 1) * HALF)
-            for t in range(PACK):
-                cols = slice(t * P, (t + 1) * P)
-                for s in range(PASSES):
+        def first_layer_pass(accs, weights, e, s):
+            for u in range(2):
+                slots = slice(u * HALF, (u + 1) * HALF)
+                for t in range(PACK):
+                    cols = slice(t * P, (t + 1) * P)
                     nc.tensor.matmul_mx(
-                        out=acc[:, t, :],
-                        lhsT=weights[s][0][:, cols].bitcast(FP8X4),
-                        lhsT_scale=weights[s][1][:, cols],
+                        out=accs[u][:, t, :],
+                        lhsT=weights[0][:, cols].bitcast(FP8X4),
+                        lhsT_scale=weights[1][:, cols],
                         rhs=slot_codes[e][:, s, slots].bitcast(FP8X4),
                         rhs_scale=slot_scales[e][PLANE * s :, slots],
-                        start=(s == 0),
-                        stop=(s == PASSES - 1),
+                        start=(s == 0 and t == 0),
+                        stop=(s == PASSES - 1 and t == PACK - 1),
                     )
 
         def hidden(h, b, sig, slots):
@@ -137,20 +137,45 @@ def tile_moe_tk_glu_sigmoid_kernel(tc, xT, w1, w3, w2, gate, offs, pos1, pos2, p
             )
             quantize(h_codes[:, slots], h_scales[:, slots], h.rearrange("p c t -> p (c t)"))
 
-        def second_layer(acc, pieces, copy):
-            first, last = pieces[0][1].start, pieces[-1][1].stop
-            for e, slots in pieces:
+        def gates_of(a, spent):
+            sig = []
+            for u in range(2):
+                sig_u = spent[:, 2 * u : 2 * u + 2, 0 : 2 * HALF].rearrange("p g (c t) -> p g c t", t=PACK)
+                nc.scalar.activation(out=sig_u, in_=a[u][:].rearrange("p t (g c) -> p g c t", g=2), func=SIGMOID)
+                sig.append(sig_u)
+            return sig
+
+        def gated(e, b, sig, spent):
+            for u in range(2):
+                if spent is None:
+                    h = work.tile([P, HALF, PACK], BF16, name="h", align_bytes=64)[:]
+                else:
+                    h = spent[:, u, H // 2 :].bitcast(BF16).rearrange("p (c t) -> p c t", t=PACK)
+                hidden(h, b[u], sig[u], slice(e * C + u * HALF, e * C + (u + 1) * HALF))
+
+        def quantized_w2(e, copy):
+            raw = loads.tile([P, PACK, N], F32, name="w2_raw", tag="raw", align_bytes=64)
+            nc.sync.dma_start(out=raw[:], in_=w2[e].rearrange("(p j) n -> p j n", j=PACK))
+            grouped = small.tile([P, N, PACK], BF16, name="w2_grouped", align_bytes=64)
+            interleave(copy, grouped[:], raw[:])
+            cols = slice(e * N, (e + 1) * N)
+            quantize(w2_codes[:, cols], w2_scales[:, cols], grouped[:].rearrange("p n j -> p (n j)"))
+
+        def second_layer(slots, copy, pool, tag):
+            acc = pool.tile([P, slots.stop - slots.start], F32, name="y_acc", tag=tag)
+            for e in range(slots.start // C, (slots.stop - 1) // C + 1):
                 cols = slice(e * N, (e + 1) * N)
+                first, stop = max(slots.start, e * C), min(slots.stop, (e + 1) * C)
                 nc.tensor.matmul_mx(
-                    out=acc[:, slots.start - first : slots.stop - first],
+                    out=acc[:, first - slots.start : stop - slots.start],
                     lhsT=w2_codes[:, cols].bitcast(FP8X4),
                     lhsT_scale=w2_scales[:, cols],
-                    rhs=h_codes[:, slots].bitcast(FP8X4),
-                    rhs_scale=h_scales[:, slots],
+                    rhs=h_codes[:, first:stop].bitcast(FP8X4),
+                    rhs_scale=h_scales[:, first:stop],
                     start=True,
                     stop=True,
                 )
-            copy(out=y[:, first:last], in_=acc)
+            copy(out=y[:, slots], in_=acc[:])
 
         gather_codes(0)
         gather_scales(0)
@@ -164,64 +189,34 @@ def tile_moe_tk_glu_sigmoid_kernel(tc, xT, w1, w3, w2, gate, offs, pos1, pos2, p
             if not last:
                 gather_scales(e + 1)
             w1_q.append(quantized_weights(w1, e, 1, share[1], work, "grouped", 1))
-            a = []
-            for u in range(2):
-                a_u = psum_a.tile([P, PACK, HALF], F32, name="a")
-                first_layer(a_u, w1_q, e, u)
-                a.append(a_u)
+            a = [psum_a.tile([P, PACK, HALF], F32, name="a", tag="a") for u in range(2)]
+            for s in range(PASSES):
+                first_layer_pass(a, w1_q[s], e, s)
 
             w3_q = [quantized_weights(w3, e, 0, share[2], work, "grouped", 1)]
             w3_q.append(quantized_weights(w3, e, 1, share[3], turns, "codes_turn%d" % ((e + 2) % TURNS), 2 if last else 1))
             if e + 2 < E:
                 gather_codes(e + 2)
-            b = []
-            for u in range(2):
-                b_u = psum_b.tile([P, PACK, HALF], F32, name="b")
-                first_layer(b_u, w3_q, e, u)
-                b.append(b_u)
-            spent = w3_q[PASSES - 1][2]
-            sig = []
-            for u in range(2):
-                sig_u = spent[:, 2 * u : 2 * u + 2, 0 : 2 * HALF].rearrange("p g (c t) -> p g c t", t=PACK)
-                nc.scalar.activation(out=sig_u, in_=a[u][:].rearrange("p t (g c) -> p g c t", g=2), func=SIGMOID)
-                sig.append(sig_u)
-            if not last:
-                for u in range(2):
-                    h = work.tile([P, HALF, PACK], BF16, name="h", align_bytes=64)
-                    hidden(h[:], b[u], sig[u], halves[u])
+            b = [psum_b.tile([P, PACK, HALF], F32, name="b") for u in range(2)]
+            for s in range(PASSES):
+                first_layer_pass(b, w3_q[s], e, s)
+            sig = gates_of(a, w3_q[0 if last else 1][2])
+            if e < 5:
+                gated(e, b, sig, None)
 
-        w2_grouped = []
-        for pair in range(E // 2):
-            raw = loads.tile([P, 2, PACK, N], F32, name="w2_raw", tag="raw")
-            nc.sync.dma_start(out=raw[:], in_=w2[2 * pair : 2 * pair + 2].rearrange("e (p j) n -> p e j n", j=PACK))
-            grouped = work.tile([P, 2, N, PACK], BF16, name="w2_grouped", align_bytes=64)
-            for i in range(2):
-                interleave(copy_on[W2_CAST[pair][i]], grouped[:, i, :, :], raw[:, i, :, :])
-            cols = slice(2 * pair * N, (2 * pair + 2) * N)
-            quantize(w2_codes[:, cols], w2_scales[:, cols], grouped[:].rearrange("p e n j -> p (e n j)"))
-            w2_grouped.append(grouped)
-        for u in range(2):
-            if u == 0:
-                h = w2_grouped[0][:, 0, :, :]
-            else:
-                h = work.tile([P, HALF, PACK], BF16, name="h", align_bytes=64)[:]
-            hidden(h, b[u], sig[u], halves[u])
-            y_half = psum_y.tile([P, HALF], F32, name="y_half")
-            second_layer(y_half[:], [(E - 1, halves[u])], nc.vector.tensor_copy)
-        for u in range(2):
-            pieces = [(e, slice(e * C, (e + 1) * C)) for e in (2 * u, 2 * u + 1)]
-            second_layer(b[u][:].rearrange("p t c -> p (t c)"), pieces, nc.scalar.copy)
-        y_whole = psum_y.tile([P, C], F32, name="y_whole")
-        second_layer(y_whole[:], [(E - 2, slice((E - 2) * C, (E - 1) * C))], nc.scalar.copy)
+        for e in [E - 1] + list(range(E - 1)):
+            quantized_w2(e, nc.vector.tensor_copy if e >= E - 2 else nc.scalar.copy)
+        gated(E - 1, b, sig, None)
+        second_layer(slice(0, 2 * C), nc.scalar.copy, psum_y, "y_acc")
+        for e in range(2, E):
+            second_layer(slice(e * C, (e + 1) * C), nc.vector.tensor_copy if e == E - 2 else nc.scalar.copy, psum_a if e == E - 1 else psum_y, "a" if e == E - 1 else "y_acc")
 
-        token_slot = []
+        token_slot, gates = [], []
         for r, pos in enumerate((pos1, pos2, pos3)):
             tile = held.tile([P, T // 16], U16, name="token_slot%d" % r)
             nc.sync.dma_start(tile[:], pos)
             token_slot.append(tile)
-        gates = []
-        for r in range(TOP):
-            gate_r = loads.tile([P, T], F32, name="gate_r", tag="raw")
+            gate_r = loads.tile([P, T], F32, name="gate_r", tag="raw", align_bytes=64)
             nc.sync.dma_start(out=gate_r[:], in_=gate[r])
             gates.append(gate_r)
 

@@ -24,8 +24,8 @@ HALF = C // 2
 PLANE = 4
 TURNS = 3
 X_SCALAR_COLUMNS = 176
-SCALAR_SHARE = (80, 96, 64, 96)
-SCALAR_SHARE_LAST = (64, 64, 48, 44)
+SCALAR_SHARE = (72, 96, 72, 96)
+SCALAR_SHARE_LAST = (80, 80, 48, 48)
 EARLY_W2 = 0
 COMBINE = (256, 128, 128)
 
@@ -84,7 +84,6 @@ def tile_moe_tk_glu_sigmoid_kernel(tc, xT, w1, w3, w2, gate, offs, pos1, pos2, p
             quantize(codes[:], x_scales[PLANE * s :, :], x_grouped[:].rearrange("p c j -> p (c j)"))
             x_codes.append(codes)
 
-        y = held.tile([P, E * C], F32, name="y")
         h_codes = held.tile([P, E * C], U32, name="h_codes", align_bytes=64)
         h_scales = held.tile([P, E * C], U8, name="h_scales", align_bytes=64)
         w2_codes = held.tile([P, E * N], U32, name="w2_codes", align_bytes=64)
@@ -133,15 +132,15 @@ def tile_moe_tk_glu_sigmoid_kernel(tc, xT, w1, w3, w2, gate, offs, pos1, pos2, p
 
         def hidden(h, b, sig, slots):
             nc.vector.tensor_tensor(
-                h.rearrange("p (g c) t -> p g c t", g=2), b[:].rearrange("p t (g c) -> p g c t", g=2), sig, MULT
+                h.rearrange("p (g c) t -> p g c t", g=PACK), b[:].rearrange("p t (g c) -> p g c t", g=PACK), sig, MULT
             )
             quantize(h_codes[:, slots], h_scales[:, slots], h.rearrange("p c t -> p (c t)"))
 
         def gates_of(a, spent):
             sig = []
             for u in range(2):
-                sig_u = spent[:, 2 * u : 2 * u + 2, 0 : 2 * HALF].rearrange("p g (c t) -> p g c t", t=PACK)
-                nc.scalar.activation(out=sig_u, in_=a[u][:].rearrange("p t (g c) -> p g c t", g=2), func=SIGMOID)
+                sig_u = spent[:, :, u * HALF : (u + 1) * HALF].rearrange("p g (c t) -> p g c t", t=PACK)
+                nc.scalar.activation(out=sig_u, in_=a[u][:].rearrange("p t (g c) -> p g c t", g=PACK), func=SIGMOID)
                 sig.append(sig_u)
             return sig
 
@@ -153,8 +152,8 @@ def tile_moe_tk_glu_sigmoid_kernel(tc, xT, w1, w3, w2, gate, offs, pos1, pos2, p
                     h = spent[:, u, H // 2 :].bitcast(BF16).rearrange("p (c t) -> p c t", t=PACK)
                 hidden(h, b[u], sig[u], slice(e * C + u * HALF, e * C + (u + 1) * HALF))
 
-        def quantized_w2(e, copy):
-            raw = loads.tile([P, PACK, N], F32, name="w2_raw", tag="raw", align_bytes=64)
+        def quantized_w2(e, copy, pool, tag):
+            raw = pool.tile([P, PACK, N], F32, name="w2_raw", tag=tag, align_bytes=64)
             nc.sync.dma_start(out=raw[:], in_=w2[e].rearrange("(p j) n -> p j n", j=PACK))
             grouped = small.tile([P, N, PACK], BF16, name="w2_grouped", align_bytes=64)
             interleave(copy, grouped[:], raw[:])
@@ -193,7 +192,7 @@ def tile_moe_tk_glu_sigmoid_kernel(tc, xT, w1, w3, w2, gate, offs, pos1, pos2, p
             for s in range(PASSES):
                 first_layer_pass(a, w1_q[s], e, s)
 
-            w3_q = [quantized_weights(w3, e, 0, share[2], work, "grouped", 1)]
+            w3_q = [quantized_weights(w3, e, 0, share[2], *((turns, "result_turn") if last else (work, "grouped")), 1)]
             w3_q.append(quantized_weights(w3, e, 1, share[3], turns, "codes_turn%d" % ((e + 2) % TURNS), 2 if last else 1))
             if e + 2 < E:
                 gather_codes(e + 2)
@@ -205,20 +204,21 @@ def tile_moe_tk_glu_sigmoid_kernel(tc, xT, w1, w3, w2, gate, offs, pos1, pos2, p
                 gated(e, b, sig, None)
 
         for e in [E - 1] + list(range(E - 1)):
-            quantized_w2(e, nc.vector.tensor_copy if e >= E - 2 else nc.scalar.copy)
+            quantized_w2(e, nc.vector.tensor_copy if e == E - 1 else nc.scalar.copy, *((turns, "result_turn") if e == E - 2 else (loads, "raw")))
+        y = turns.tile([P, E * C], F32, name="y", tag="result_turn", align_bytes=64)
         gated(E - 1, b, sig, None)
         second_layer(slice(0, 2 * C), nc.scalar.copy, psum_y, "y_acc")
         for e in range(2, E):
-            second_layer(slice(e * C, (e + 1) * C), nc.vector.tensor_copy if e == E - 2 else nc.scalar.copy, psum_a if e == E - 1 else psum_y, "a" if e == E - 1 else "y_acc")
+            second_layer(slice(e * C, (e + 1) * C), nc.vector.tensor_copy if e >= E - 2 else nc.scalar.copy, psum_a if e == E - 1 else psum_y, "a" if e == E - 1 else "y_acc")
 
+        gate_rows = turns.tile([P, TOP, T], F32, name="gate_rows", tag="codes_turn%d" % ((E + 1) % TURNS), align_bytes=64)
         token_slot, gates = [], []
         for r, pos in enumerate((pos1, pos2, pos3)):
             tile = held.tile([P, T // 16], U16, name="token_slot%d" % r)
             nc.sync.dma_start(tile[:], pos)
             token_slot.append(tile)
-            gate_r = loads.tile([P, T], F32, name="gate_r", tag="raw", align_bytes=64)
-            nc.sync.dma_start(out=gate_r[:], in_=gate[r])
-            gates.append(gate_r)
+            nc.sync.dma_start(out=gate_rows[:, r, :], in_=gate[r])
+            gates.append(gate_rows[:, r, :])
 
         products = held.tile([P, TOP, T], F32, name="products")
         partial = held.tile([P, T], F32, name="partial")

@@ -24,7 +24,7 @@ HALF = C // 2
 PLANE = 4
 TURNS = 3
 X_SCALAR_COLUMNS = 176
-SCALAR_SHARE = (72, 96, 72, 96)
+SCALAR_SHARE = (88, 96, 88, 96)
 SCALAR_SHARE_LAST = (80, 80, 48, 48)
 EARLY_W2 = 0
 COMBINE = (256, 128, 128)

@@ -1,6 +1,7 @@
 from contextlib import ExitStack
 
 import concourse.mybir as mybir
+from concourse.masks import make_identity
 
 K, T, E, C, H, N = 1024, 512, 6, 256, 512, 128
 TOP = 3
@@ -24,7 +25,7 @@ HALF = C // 2
 PLANE = 4
 TURNS = 3
 X_SCALAR_COLUMNS = 176
-SCALAR_SHARE = (88, 96, 88, 96)
+SCALAR_SHARE = (96, 96, 96, 96)
 SCALAR_SHARE_LAST = (80, 80, 48, 48)
 EARLY_W2 = 0
 COMBINE = (256, 128, 128)
@@ -84,6 +85,8 @@ def tile_moe_tk_glu_sigmoid_kernel(tc, xT, w1, w3, w2, gate, offs, pos1, pos2, p
             quantize(codes[:], x_scales[PLANE * s :, :], x_grouped[:].rearrange("p c j -> p (c j)"))
             x_codes.append(codes)
 
+        identity = held.tile([P, P], F32, name="identity")
+        make_identity(nc, identity[:])
         h_codes = held.tile([P, E * C], U32, name="h_codes", align_bytes=64)
         h_scales = held.tile([P, E * C], U8, name="h_scales", align_bytes=64)
         w2_codes = held.tile([P, E * N], U32, name="w2_codes", align_bytes=64)
@@ -196,7 +199,7 @@ def tile_moe_tk_glu_sigmoid_kernel(tc, xT, w1, w3, w2, gate, offs, pos1, pos2, p
             w3_q.append(quantized_weights(w3, e, 1, share[3], turns, "codes_turn%d" % ((e + 2) % TURNS), 2 if last else 1))
             if e + 2 < E:
                 gather_codes(e + 2)
-            b = [psum_b.tile([P, PACK, HALF], F32, name="b") for u in range(2)]
+            b = [psum_b.tile([P, PACK, HALF], F32, name="b", tag="b") for u in range(2)]
             for s in range(PASSES):
                 first_layer_pass(b, w3_q[s], e, s)
             sig = gates_of(a, w3_q[0 if last else 1][2])
@@ -221,25 +224,41 @@ def tile_moe_tk_glu_sigmoid_kernel(tc, xT, w1, w3, w2, gate, offs, pos1, pos2, p
             gates.append(gate_rows[:, r, :])
 
         products = held.tile([P, TOP, T], F32, name="products")
-        partial = held.tile([P, T], F32, name="partial")
+        turned = held.tile([P, T], F32, name="turned")
         total = held.tile([P, T], F32, name="total")
-        for r in range(TOP - 1):
-            nc.vector.tensor_tensor(products[:, r, :], y[:].indirect(token_slot[r][:]), gates[r][:], MULT)
 
-        def finish(tokens):
-            nc.vector.tensor_tensor(total[:, tokens], partial[:, tokens], products[:, TOP - 1, tokens], ADD)
-            nc.sync.dma_start(out=out[:, tokens], in_=total[:, tokens])
+        def product(r, tokens):
+            slots_of = token_slot[r][:, tokens.start // 16 : tokens.stop // 16]
+            nc.vector.tensor_tensor(products[:, r, tokens], y[:].indirect(slots_of), gates[r][:, tokens], MULT)
 
+        def first_two(tokens):
+            blocks = range(tokens.start, tokens.stop, P)
+            summed = psum_y.tile([P, tokens.stop - tokens.start], F32, name="summed", tag="y_acc")
+            for r in range(2):
+                product(r, tokens)
+                for t0 in blocks:
+                    nc.tensor.matmul(
+                        summed[:, t0 - tokens.start : t0 - tokens.start + P],
+                        products[:, r, t0 : t0 + P],
+                        identity[:],
+                        is_transpose=True,
+                        start=(r == 0 and t0 == blocks[0]),
+                        stop=(r == 1 and t0 == blocks[-1]),
+                    )
+            nc.scalar.copy(out=turned[:, tokens], in_=summed[:])
+            back = psum_b.tile([P, tokens.stop - tokens.start], F32, name="back", tag="b")
+            for t0 in blocks:
+                nc.tensor.transpose(back[:, t0 - tokens.start : t0 - tokens.start + P], turned[:, t0 : t0 + P], identity[:])
+            return back
+
+        partial = [first_two(slice(half * T // 2, (half + 1) * T // 2)) for half in range(2)]
+        for half in range(2):
+            product(TOP - 1, slice(half * T // 2, (half + 1) * T // 2))
         t0 = 0
-        waiting = None
         for width in COMBINE:
             tokens = slice(t0, t0 + width)
-            slots_of = token_slot[TOP - 1][:, t0 // 16 : (t0 + width) // 16]
-            nc.vector.tensor_tensor(products[:, TOP - 1, tokens], y[:].indirect(slots_of), gates[TOP - 1][:, tokens], MULT)
-            if waiting is None:
-                nc.vector.tensor_tensor(partial[:], products[:, 0, :], products[:, 1, :], ADD)
-            else:
-                finish(waiting)
-            waiting = tokens
+            half = t0 // (T // 2)
+            inside = slice(t0 - half * T // 2, t0 + width - half * T // 2)
+            nc.vector.tensor_tensor(total[:, tokens], partial[half][:, inside], products[:, TOP - 1, tokens], ADD)
+            nc.sync.dma_start(out=out[:, tokens], in_=total[:, tokens])
             t0 += width
-        finish(waiting)

@@ -61,8 +61,8 @@ def tile_moe_tk_glu_sigmoid_kernel(tc, xT, w1, w3, w2, gate, offs, pos1, pos2, p
 
         def interleave_permuted(copy, grouped, raw, m0, m1):
             copy(
-                out=grouped[:, :, m0:m1, :].rearrange("p t m j -> p m j t"),
-                in_=raw[:, :, PACK * m0 : PACK * m1].rearrange("p j (m t) -> p m j t", t=PACK),
+                out=grouped[:, :, m0:m1, :].rearrange("p t m (a b) -> p m a t b", b=2),
+                in_=raw[:, :, PACK * m0 : PACK * m1].rearrange("p (a b) (m t) -> p m a t b", b=2, t=PACK),
             )
 
         warm = held.tile([P, 8], F32, name="warm")

@@ -19,16 +19,20 @@ SIGMOID = mybir.ActivationFunctionType.Sigmoid
 
 P = 128
 PACK = 4
+LINE = 4
+GROUP = 16
 K_PASS = P * PACK
 PASSES = K // K_PASS
 HALF = C // 2
-PLANE = 4
+SCALE_ROWS = 4
 TURNS = 3
+STAGING = 14
+ROUNDED = 4
+QUANTISED = 8
+
 X_SCALAR_COLUMNS = 176
-SCALAR_SHARE = (96, 96, 96, 96)
+SCALAR_SHARE = 96
 SCALAR_SHARE_LAST = (80, 80, 48, 48)
-EARLY_W2 = 0
-COMBINE = (256, 128, 128)
 
 
 def tile_moe_tk_glu_sigmoid_kernel(tc, xT, w1, w3, w2, gate, offs, pos1, pos2, pos3, out):
@@ -37,9 +41,9 @@ def tile_moe_tk_glu_sigmoid_kernel(tc, xT, w1, w3, w2, gate, offs, pos1, pos2, p
     with ExitStack() as ctx:
         held = ctx.enter_context(tc.tile_pool(name="held", bufs=1))
         turns = ctx.enter_context(tc.tile_pool(name="turns", bufs=1))
-        loads = ctx.enter_context(tc.tile_pool(name="loads", bufs=14))
-        work = ctx.enter_context(tc.tile_pool(name="work", bufs=4))
-        quant = ctx.enter_context(tc.tile_pool(name="quant", bufs=8))
+        loads = ctx.enter_context(tc.tile_pool(name="loads", bufs=STAGING))
+        work = ctx.enter_context(tc.tile_pool(name="work", bufs=ROUNDED))
+        quant = ctx.enter_context(tc.tile_pool(name="quant", bufs=QUANTISED))
         small = ctx.enter_context(tc.tile_pool(name="small", bufs=E))
         psum_a = ctx.enter_context(tc.psum_pool(name="psum_a", bufs=2))
         psum_b = ctx.enter_context(tc.psum_pool(name="psum_b", bufs=2))
@@ -55,14 +59,14 @@ def tile_moe_tk_glu_sigmoid_kernel(tc, xT, w1, w3, w2, gate, offs, pos1, pos2, p
 
         def interleave(copy, grouped, raw):
             copy(
-                out=grouped.rearrange("p (c i) j -> p c j i", i=4),
-                in_=raw.rearrange("p j (c i) -> p c j i", i=4),
+                out=grouped.rearrange("p (c i) j -> p c j i", i=LINE),
+                in_=raw.rearrange("p j (c i) -> p c j i", i=LINE),
             )
 
         def interleave_permuted(copy, grouped, raw, m0, m1):
             copy(
-                out=grouped[:, :, m0:m1, :].rearrange("p t m (a b) -> p m a t b", b=2),
-                in_=raw[:, :, PACK * m0 : PACK * m1].rearrange("p (a b) (m t) -> p m a t b", b=2, t=PACK),
+                out=grouped[:, :, m0:m1, :].rearrange("p t m (pair row) -> p m pair t row", row=2),
+                in_=raw[:, :, PACK * m0 : PACK * m1].rearrange("p (pair row) (m t) -> p m pair t row", row=2, t=PACK),
             )
 
         warm = held.tile([P, 8], F32, name="warm")
@@ -71,7 +75,7 @@ def tile_moe_tk_glu_sigmoid_kernel(tc, xT, w1, w3, w2, gate, offs, pos1, pos2, p
         nc.scalar.activation(out=warm_out[:], in_=warm[:], func=SIGMOID)
 
         x_raw = [load_rows(xT[s * K_PASS : (s + 1) * K_PASS, :]) for s in range(PASSES)]
-        slot_token = held.tile([P, E * C // 16], U16, name="slot_token")
+        slot_token = held.tile([P, E * C // GROUP], U16, name="slot_token")
         nc.sync.dma_start(slot_token[:], offs)
 
         x_codes = []
@@ -82,7 +86,7 @@ def tile_moe_tk_glu_sigmoid_kernel(tc, xT, w1, w3, w2, gate, offs, pos1, pos2, p
             x_grouped = work.tile([P, T, PACK], BF16, name="x_grouped", tag="grouped", align_bytes=64)
             for copy, cols in ((nc.scalar.copy, slice(0, X_SCALAR_COLUMNS)), (nc.vector.tensor_copy, slice(X_SCALAR_COLUMNS, T))):
                 interleave(copy, x_grouped[:, cols, :], x_raw[s][:, :, cols])
-            quantize(codes[:], x_scales[PLANE * s :, :], x_grouped[:].rearrange("p c j -> p (c j)"))
+            quantize(codes[:], x_scales[SCALE_ROWS * s :, :], x_grouped[:].rearrange("p c j -> p (c j)"))
             x_codes.append(codes)
 
         identity = held.tile([P, P], F32, name="identity")
@@ -93,19 +97,25 @@ def tile_moe_tk_glu_sigmoid_kernel(tc, xT, w1, w3, w2, gate, offs, pos1, pos2, p
         w2_scales = held.tile([P, E * N], U8, name="w2_scales", align_bytes=64)
         slot_codes, slot_scales = {}, {}
 
+        def codes_turn(e):
+            return "codes_turn%d" % (e % TURNS)
+
+        def scales_turn(e):
+            return "scales_turn%d" % (e % TURNS)
+
         def picks(e):
-            return slot_token[:, e * C // 16 : (e + 1) * C // 16]
+            return slot_token[:, e * C // GROUP : (e + 1) * C // GROUP]
 
         def gather_codes(e):
-            slot_codes[e] = turns.tile([P, PASSES, C], U32, name="slot_codes", tag="codes_turn%d" % (e % TURNS), align_bytes=64)
+            slot_codes[e] = turns.tile([P, PASSES, C], U32, name="slot_codes", tag=codes_turn(e), align_bytes=64)
             for s in range(PASSES):
                 nc.vector.tensor_copy(slot_codes[e][:, s, :], x_codes[s][:].indirect(picks(e)))
 
         def gather_scales(e):
-            slot_scales[e] = turns.tile([P, C], U8, name="slot_scales", tag="scales_turn%d" % (e % TURNS), align_bytes=64)
+            slot_scales[e] = turns.tile([P, C], U8, name="slot_scales", tag=scales_turn(e), align_bytes=64)
             nc.vector.tensor_copy(slot_scales[e][:], x_scales[:].indirect(picks(e)))
 
-        def quantized_weights(w, e, s, share, pool, tag, pieces):
+        def quantized_weights(w, e, s, share, pool, tag, pieces=1):
             raw = load_rows(w[e, s * K_PASS : (s + 1) * K_PASS, :])
             grouped = pool.tile([P, PACK, P, PACK], BF16, name="w_grouped", tag=tag, align_bytes=64)
             interleave_permuted(nc.scalar.copy, grouped, raw, 0, share)
@@ -118,147 +128,162 @@ def tile_moe_tk_glu_sigmoid_kernel(tc, xT, w1, w3, w2, gate, offs, pos1, pos2, p
                 quantize(codes[:, cols], scales[:, cols], grouped[:, t : t + step, :, :].rearrange("p t m j -> p (t m j)"))
             return codes, scales, raw
 
-        def first_layer_pass(accs, weights, e, s):
+        def first_layer_pass(banks, weights, e, s):
+            codes, scales = weights[0], weights[1]
             for u in range(2):
                 slots = slice(u * HALF, (u + 1) * HALF)
                 for t in range(PACK):
                     cols = slice(t * P, (t + 1) * P)
                     nc.tensor.matmul_mx(
-                        out=accs[u][:, t, :],
-                        lhsT=weights[0][:, cols].bitcast(FP8X4),
-                        lhsT_scale=weights[1][:, cols],
+                        out=banks[u][:, t, :],
+                        lhsT=codes[:, cols].bitcast(FP8X4),
+                        lhsT_scale=scales[:, cols],
                         rhs=slot_codes[e][:, s, slots].bitcast(FP8X4),
-                        rhs_scale=slot_scales[e][PLANE * s :, slots],
+                        rhs_scale=slot_scales[e][SCALE_ROWS * s :, slots],
                         start=(s == 0 and t == 0),
                         stop=(s == PASSES - 1 and t == PACK - 1),
                     )
 
-        def hidden(h, b, sig, slots):
-            nc.vector.tensor_tensor(
-                h.rearrange("p (g c) t -> p g c t", g=PACK), b[:].rearrange("p t (g c) -> p g c t", g=PACK), sig, MULT
-            )
-            quantize(h_codes[:, slots], h_scales[:, slots], h.rearrange("p c t -> p (c t)"))
-
-        def gates_of(a, spent):
-            sig = []
-            for u in range(2):
-                sig_u = spent[:, :, u * HALF : (u + 1) * HALF].rearrange("p g (c t) -> p g c t", t=PACK)
-                nc.scalar.activation(out=sig_u, in_=a[u][:].rearrange("p t (g c) -> p g c t", g=PACK), func=SIGMOID)
-                sig.append(sig_u)
+        def sigmoid_over(bank, spent, column):
+            sig = spent[:, :, column : column + HALF].rearrange("p g (c t) -> p g c t", t=PACK)
+            nc.scalar.activation(out=sig, in_=bank[:].rearrange("p t (g c) -> p g c t", g=PACK), func=SIGMOID)
             return sig
 
-        def gated(e, b, sig, spent):
-            for u in range(2):
-                if spent is None:
-                    h = work.tile([P, HALF, PACK], BF16, name="h", align_bytes=64)[:]
-                else:
-                    h = spent[:, u, H // 2 :].bitcast(BF16).rearrange("p (c t) -> p c t", t=PACK)
-                hidden(h, b[u], sig[u], slice(e * C + u * HALF, e * C + (u + 1) * HALF))
+        def hidden(bank, sig):
+            h = work.tile([P, HALF, PACK], BF16, name="h", align_bytes=64)
+            nc.vector.tensor_tensor(
+                h[:].rearrange("p (g c) t -> p g c t", g=PACK), bank[:].rearrange("p t (g c) -> p g c t", g=PACK), sig, MULT
+            )
+            return h
 
-        def quantized_w2(e, copy, pool, tag):
+        def quantize_hidden(h, e, u):
+            slots = slice(e * C + u * HALF, e * C + (u + 1) * HALF)
+            quantize(h_codes[:, slots], h_scales[:, slots], h[:].rearrange("p c t -> p (c t)"))
+
+        def rounded_w2(e, copy, pool, tag):
             raw = pool.tile([P, PACK, N], F32, name="w2_raw", tag=tag, align_bytes=64)
             nc.sync.dma_start(out=raw[:], in_=w2[e].rearrange("(p j) n -> p j n", j=PACK))
             grouped = small.tile([P, N, PACK], BF16, name="w2_grouped", align_bytes=64)
             interleave(copy, grouped[:], raw[:])
-            cols = slice(e * N, (e + 1) * N)
-            quantize(w2_codes[:, cols], w2_scales[:, cols], grouped[:].rearrange("p n j -> p (n j)"))
+            return grouped
 
-        def second_layer(slots, copy, pool, tag):
-            acc = pool.tile([P, slots.stop - slots.start], F32, name="y_acc", tag=tag)
-            for e in range(slots.start // C, (slots.stop - 1) // C + 1):
+        def quantize_w2(e):
+            cols = slice(e * N, (e + 1) * N)
+            quantize(w2_codes[:, cols], w2_scales[:, cols], w2_grouped[e][:].rearrange("p n j -> p (n j)"))
+
+        def second_layer(experts, copy, pool, tag):
+            acc = pool.tile([P, len(experts) * C], F32, name="y_acc", tag=tag)
+            for place, e in enumerate(experts):
                 cols = slice(e * N, (e + 1) * N)
-                first, stop = max(slots.start, e * C), min(slots.stop, (e + 1) * C)
+                slots = slice(e * C, (e + 1) * C)
                 nc.tensor.matmul_mx(
-                    out=acc[:, first - slots.start : stop - slots.start],
+                    out=acc[:, place * C : (place + 1) * C],
                     lhsT=w2_codes[:, cols].bitcast(FP8X4),
                     lhsT_scale=w2_scales[:, cols],
-                    rhs=h_codes[:, first:stop].bitcast(FP8X4),
-                    rhs_scale=h_scales[:, first:stop],
+                    rhs=h_codes[:, slots].bitcast(FP8X4),
+                    rhs_scale=h_scales[:, slots],
                     start=True,
                     stop=True,
                 )
-            copy(out=y[:, slots], in_=acc[:])
+            copy(out=y[:, experts[0] * C : (experts[-1] + 1) * C], in_=acc[:])
 
+        last = E - 1
         gather_codes(0)
         gather_scales(0)
         gather_codes(1)
         for e in range(E):
-            last = e == E - 1
-            share = SCALAR_SHARE_LAST if last else SCALAR_SHARE
-            halves = [slice(e * C + u * HALF, e * C + (u + 1) * HALF) for u in range(2)]
+            share = SCALAR_SHARE_LAST if e == last else (SCALAR_SHARE,) * (2 * PASSES)
 
-            w1_q = [quantized_weights(w1, e, 0, share[0], turns, "scales_turn%d" % ((e + 1) % TURNS), 1)]
-            if not last:
+            w1_q = [quantized_weights(w1, e, 0, share[0], turns, scales_turn(e + 1))]
+            if e < last:
                 gather_scales(e + 1)
-            w1_q.append(quantized_weights(w1, e, 1, share[1], work, "grouped", 1))
+            w1_q.append(quantized_weights(w1, e, 1, share[1], work, "grouped"))
             a = [psum_a.tile([P, PACK, HALF], F32, name="a", tag="a") for u in range(2)]
             for s in range(PASSES):
                 first_layer_pass(a, w1_q[s], e, s)
 
-            w3_q = [quantized_weights(w3, e, 0, share[2], *((turns, "result_turn") if last else (work, "grouped")), 1)]
-            w3_q.append(quantized_weights(w3, e, 1, share[3], turns, "codes_turn%d" % ((e + 2) % TURNS), 2 if last else 1))
+            pool, tag = (turns, "result_turn") if e == last else (work, "grouped")
+            w3_q = [quantized_weights(w3, e, 0, share[2], pool, tag)]
+            w3_q.append(quantized_weights(w3, e, 1, share[3], turns, codes_turn(e + 2), 2 if e == last else 1))
             if e + 2 < E:
                 gather_codes(e + 2)
             b = [psum_b.tile([P, PACK, HALF], F32, name="b", tag="b") for u in range(2)]
             for s in range(PASSES):
                 first_layer_pass(b, w3_q[s], e, s)
-            sig = gates_of(a, w3_q[0 if last else 1][2])
-            if e < 5:
-                gated(e, b, sig, None)
+            if e < last:
+                sig = [sigmoid_over(a[u], w3_q[1][2], u * HALF) for u in range(2)]
+                for u in range(2):
+                    quantize_hidden(hidden(b[u], sig[u]), e, u)
+            else:
+                sig = [sigmoid_over(a[u], w3_q[u][2], 0) for u in range(2)]
 
-        for e in [E - 1] + list(range(E - 1)):
-            quantized_w2(e, nc.vector.tensor_copy if e == E - 1 else nc.scalar.copy, *((turns, "result_turn") if e == E - 2 else (loads, "raw")))
+        arrival = [last] + list(range(last))
+        w2_grouped = {}
+        for e in arrival:
+            copy = nc.vector.tensor_copy if e in arrival[:2] else nc.scalar.copy
+            pool, tag = (turns, "result_turn") if e == arrival[-1] else (loads, "raw")
+            w2_grouped[e] = rounded_w2(e, copy, pool, tag)
         y = turns.tile([P, E * C], F32, name="y", tag="result_turn", align_bytes=64)
-        gated(E - 1, b, sig, None)
-        second_layer(slice(0, 2 * C), nc.scalar.copy, psum_y, "y_acc")
-        for e in range(2, E):
-            second_layer(slice(e * C, (e + 1) * C), nc.vector.tensor_copy if e >= E - 2 else nc.scalar.copy, psum_a if e == E - 1 else psum_y, "a" if e == E - 1 else "y_acc")
 
-        gate_rows = turns.tile([P, TOP, T], F32, name="gate_rows", tag="codes_turn%d" % ((E + 1) % TURNS), align_bytes=64)
-        token_slot, gates = [], []
+        quantize_w2(arrival[0])
+        quantize_w2(arrival[1])
+        h_last = [hidden(b[0], sig[0])]
+        quantize_w2(arrival[2])
+        h_last.append(hidden(b[1], sig[1]))
+        for u in range(2):
+            quantize_hidden(h_last[u], last, u)
+            quantize_w2(arrival[3 + u])
+        quantize_w2(arrival[-1])
+
+        second_layer((0, 1), nc.scalar.copy, psum_y, "y_acc")
+        second_layer((2,), nc.scalar.copy, psum_y, "y_acc")
+        second_layer((3,), nc.scalar.copy, psum_y, "y_acc")
+        second_layer((arrival[-1],), nc.vector.tensor_copy, psum_y, "y_acc")
+        second_layer((last,), nc.vector.tensor_copy, psum_a, "a")
+
+        gates = turns.tile([P, TOP, T], F32, name="gate_rows", tag=codes_turn(last + 2), align_bytes=64)
+        token_slot = []
         for r, pos in enumerate((pos1, pos2, pos3)):
-            tile = held.tile([P, T // 16], U16, name="token_slot%d" % r)
-            nc.sync.dma_start(tile[:], pos)
-            token_slot.append(tile)
-            nc.sync.dma_start(out=gate_rows[:, r, :], in_=gate[r])
-            gates.append(gate_rows[:, r, :])
+            slot_list = held.tile([P, T // GROUP], U16, name="token_slot%d" % r)
+            nc.sync.dma_start(slot_list[:], pos)
+            token_slot.append(slot_list)
+        early, late = slice(0, T // 2), slice(T // 2, T)
+        for tokens in (early, late):
+            nc.sync.dma_start(out=gates[:, :, tokens], in_=gate[:, :, tokens].rearrange("r p t -> p r t"))
 
         products = held.tile([P, TOP, T], F32, name="products")
-        turned = held.tile([P, T], F32, name="turned")
+        two_sum = held.tile([P, T], F32, name="turned")
         total = held.tile([P, T], F32, name="total")
 
         def product(r, tokens):
-            slots_of = token_slot[r][:, tokens.start // 16 : tokens.stop // 16]
-            nc.vector.tensor_tensor(products[:, r, tokens], y[:].indirect(slots_of), gates[r][:, tokens], MULT)
+            slots_of = token_slot[r][:, tokens.start // GROUP : tokens.stop // GROUP]
+            nc.vector.tensor_tensor(products[:, r, tokens], y[:].indirect(slots_of), gates[:, r, tokens], MULT)
 
-        def first_two(tokens):
-            blocks = range(tokens.start, tokens.stop, P)
-            summed = psum_y.tile([P, tokens.stop - tokens.start], F32, name="summed", tag="y_acc")
-            for r in range(2):
-                product(r, tokens)
-                for t0 in blocks:
-                    nc.tensor.matmul(
-                        summed[:, t0 - tokens.start : t0 - tokens.start + P],
-                        products[:, r, t0 : t0 + P],
-                        identity[:],
-                        is_transpose=True,
-                        start=(r == 0 and t0 == blocks[0]),
-                        stop=(r == 1 and t0 == blocks[-1]),
-                    )
-            nc.scalar.copy(out=turned[:, tokens], in_=summed[:])
-            back = psum_b.tile([P, tokens.stop - tokens.start], F32, name="back", tag="b")
-            for t0 in blocks:
-                nc.tensor.transpose(back[:, t0 - tokens.start : t0 - tokens.start + P], turned[:, t0 : t0 + P], identity[:])
-            return back
+        blocks = [slice(t0, t0 + P) for t0 in range(early.start, early.stop, P)]
+        summed = psum_y.tile([P, T // 2], F32, name="summed", tag="y_acc")
+        for r in range(2):
+            product(r, early)
+            for block in blocks:
+                nc.tensor.matmul(
+                    summed[:, block],
+                    products[:, r, block],
+                    identity[:],
+                    is_transpose=True,
+                    start=(r == 0 and block == blocks[0]),
+                    stop=(r == 1 and block == blocks[-1]),
+                )
+        nc.scalar.copy(out=two_sum[:, early], in_=summed[:])
+        back = psum_b.tile([P, T // 2], F32, name="back", tag="b")
+        for block in blocks:
+            nc.tensor.transpose(back[:, block], two_sum[:, block], identity[:])
+        product(TOP - 1, early)
 
-        partial = [first_two(slice(half * T // 2, (half + 1) * T // 2)) for half in range(2)]
-        for half in range(2):
-            product(TOP - 1, slice(half * T // 2, (half + 1) * T // 2))
-        t0 = 0
-        for width in COMBINE:
-            tokens = slice(t0, t0 + width)
-            half = t0 // (T // 2)
-            inside = slice(t0 - half * T // 2, t0 + width - half * T // 2)
-            nc.vector.tensor_tensor(total[:, tokens], partial[half][:, inside], products[:, TOP - 1, tokens], ADD)
+        for r in range(TOP):
+            product(r, late)
+        nc.vector.tensor_tensor(two_sum[:, late], products[:, 0, late], products[:, 1, late], ADD)
+        nc.vector.tensor_tensor(total[:, early], back[:], products[:, TOP - 1, early], ADD)
+        nc.sync.dma_start(out=out[:, early], in_=total[:, early])
+        for t0 in range(late.start, late.stop, P):
+            tokens = slice(t0, t0 + P)
+            nc.vector.tensor_tensor(total[:, tokens], two_sum[:, tokens], products[:, TOP - 1, tokens], ADD)
             nc.sync.dma_start(out=out[:, tokens], in_=total[:, tokens])
-            t0 += width

@@ -211,9 +211,10 @@ def tile_moe_tk_glu_sigmoid_kernel(tc, xT, w1, w3, w2, gate, offs, pos1, pos2, p
             for s in range(PASSES):
                 first_layer_pass(b, w3_q[s], e, s)
             if e < last:
-                sig = [sigmoid_over(a[u], w3_q[1][2], u * HALF) for u in range(2)]
+                sig = [sigmoid_over(a[0], w3_q[1][2], H - HALF), sigmoid_over(a[1], w3_q[1][2], 0)]
+                h_pair = [hidden(b[u], sig[u]) for u in range(2)]
                 for u in range(2):
-                    quantize_hidden(hidden(b[u], sig[u]), e, u)
+                    quantize_hidden(h_pair[u], e, u)
             else:
                 sig = [sigmoid_over(a[u], w3_q[u][2], 0) for u in range(2)]
 
@@ -241,7 +242,7 @@ def tile_moe_tk_glu_sigmoid_kernel(tc, xT, w1, w3, w2, gate, offs, pos1, pos2, p
         second_layer((arrival[-1],), nc.vector.tensor_copy, psum_y, "y_acc")
         second_layer((last,), nc.vector.tensor_copy, psum_a, "a")
 
-        gates = turns.tile([P, TOP, T], F32, name="gate_rows", tag=codes_turn(last + 2), align_bytes=64)
+        gates = turns.tile([P, TOP, T], F32, name="gates", tag=codes_turn(last + 2), align_bytes=64)
         token_slot = []
         for r, pos in enumerate((pos1, pos2, pos3)):
             slot_list = held.tile([P, T // GROUP], U16, name="token_slot%d" % r)
@@ -252,7 +253,7 @@ def tile_moe_tk_glu_sigmoid_kernel(tc, xT, w1, w3, w2, gate, offs, pos1, pos2, p
             nc.sync.dma_start(out=gates[:, :, tokens], in_=gate[:, :, tokens].rearrange("r p t -> p r t"))
 
         products = held.tile([P, TOP, T], F32, name="products")
-        two_sum = held.tile([P, T], F32, name="turned")
+        two_sum = held.tile([P, T], F32, name="two_sum")
         total = held.tile([P, T], F32, name="total")
 
         def product(r, tokens):

@@ -16,6 +16,7 @@ FP8X4 = mybir.dt.float8_e4m3fn_x4
 MULT = mybir.AluOpType.mult
 ADD = mybir.AluOpType.add
 SIGMOID = mybir.ActivationFunctionType.Sigmoid
+COPY = mybir.ActivationFunctionType.Copy
 
 P = 128
 PACK = 4
@@ -243,48 +244,47 @@ def tile_moe_tk_glu_sigmoid_kernel(tc, xT, w1, w3, w2, gate, offs, pos1, pos2, p
         second_layer((last,), nc.vector.tensor_copy, psum_a, "a")
 
         gates = turns.tile([P, TOP, T], F32, name="gates", tag=codes_turn(last + 2), align_bytes=64)
+        early, late = slice(0, T // 2), slice(T // 2, T)
         token_slot = []
         for r, pos in enumerate((pos1, pos2, pos3)):
             slot_list = held.tile([P, T // GROUP], U16, name="token_slot%d" % r)
             nc.sync.dma_start(slot_list[:], pos)
             token_slot.append(slot_list)
-        early, late = slice(0, T // 2), slice(T // 2, T)
-        for tokens in (early, late):
-            nc.sync.dma_start(out=gates[:, :, tokens], in_=gate[:, :, tokens].rearrange("r p t -> p r t"))
+            nc.sync.dma_start(out=gates[:, r, early], in_=gate[r, :, early])
+        nc.sync.dma_start(out=gates[:, :, late], in_=gate[:, :, late].rearrange("r p t -> p r t"))
+
+        def results(r, tokens):
+            return y[:].indirect(token_slot[r][:, tokens.start // GROUP : tokens.stop // GROUP])
 
         products = held.tile([P, TOP, T], F32, name="products")
-        two_sum = held.tile([P, T], F32, name="two_sum")
+        picked = held.tile([P, TOP, T // 2], F32, name="picked")
+        partial = held.tile([P, T], F32, name="partial")
         total = held.tile([P, T], F32, name="total")
-
-        def product(r, tokens):
-            slots_of = token_slot[r][:, tokens.start // GROUP : tokens.stop // GROUP]
-            nc.vector.tensor_tensor(products[:, r, tokens], y[:].indirect(slots_of), gates[:, r, tokens], MULT)
-
-        blocks = [slice(t0, t0 + P) for t0 in range(early.start, early.stop, P)]
-        summed = psum_y.tile([P, T // 2], F32, name="summed", tag="y_acc")
-        for r in range(2):
-            product(r, early)
-            for block in blocks:
-                nc.tensor.matmul(
-                    summed[:, block],
-                    products[:, r, block],
-                    identity[:],
-                    is_transpose=True,
-                    start=(r == 0 and block == blocks[0]),
-                    stop=(r == 1 and block == blocks[-1]),
-                )
-        nc.scalar.copy(out=two_sum[:, early], in_=summed[:])
-        back = psum_b.tile([P, T // 2], F32, name="back", tag="b")
-        for block in blocks:
-            nc.tensor.transpose(back[:, block], two_sum[:, block], identity[:])
-        product(TOP - 1, early)
+        early_blocks = [slice(t0, t0 + P) for t0 in range(early.start, early.stop, P)]
+        late_blocks = [slice(t0, t0 + P) for t0 in range(late.start, late.stop, P)]
 
         for r in range(TOP):
-            product(r, late)
-        nc.vector.tensor_tensor(two_sum[:, late], products[:, 0, late], products[:, 1, late], ADD)
-        nc.vector.tensor_tensor(total[:, early], back[:], products[:, TOP - 1, early], ADD)
-        nc.sync.dma_start(out=out[:, early], in_=total[:, early])
-        for t0 in range(late.start, late.stop, P):
-            tokens = slice(t0, t0 + P)
-            nc.vector.tensor_tensor(total[:, tokens], two_sum[:, tokens], products[:, TOP - 1, tokens], ADD)
-            nc.sync.dma_start(out=out[:, tokens], in_=total[:, tokens])
+            nc.scalar.activation(out=picked[:, r, :], in_=results(r, late), func=COPY)
+        summed = [psum_y.tile([P, P], F32, name="summed", tag="y_acc") for block in early_blocks]
+        for r in range(TOP):
+            for tokens in early_blocks if r == TOP - 1 else [early]:
+                nc.vector.tensor_tensor(products[:, r, tokens], results(r, tokens), gates[:, r, tokens], MULT)
+            for place, block in enumerate(early_blocks):
+                nc.tensor.matmul(
+                    summed[place][:], products[:, r, block], identity[:], is_transpose=True, start=(r == 0), stop=(r == TOP - 1)
+                )
+        back = [psum_b.tile([P, P], F32, name="back", tag="b") for block in early_blocks]
+        for place, block in enumerate(early_blocks):
+            nc.scalar.copy(out=partial[:, block], in_=summed[place][:])
+            nc.tensor.transpose(back[place][:], partial[:, block], identity[:])
+        for place, block in enumerate(early_blocks):
+            nc.scalar.copy(out=total[:, block], in_=back[place][:])
+            nc.scalar.dma_start(out=out[:, block], in_=total[:, block])
+
+        nc.vector.tensor_tensor(products[:, 0:2, late], picked[:, 0:2, :], gates[:, 0:2, late], MULT)
+        nc.vector.tensor_tensor(products[:, 2, late], picked[:, 2, :], gates[:, 2, late], MULT)
+        for block in late_blocks:
+            nc.vector.tensor_tensor(partial[:, block], products[:, 0, block], products[:, 1, block], ADD)
+        for block in late_blocks:
+            nc.vector.tensor_tensor(total[:, block], partial[:, block], products[:, 2, block], ADD)
+            nc.sync.dma_start(out=out[:, block], in_=total[:, block])

from contextlib import ExitStack

import concourse.mybir as mybir
from concourse.masks import make_identity

K, T, E, C, H, N = 1024, 512, 6, 256, 512, 128
TOP = 3
FLOPS = 2 * E * C * (2 * K * H + H * N)

F32 = mybir.dt.float32
BF16 = mybir.dt.bfloat16
U32 = mybir.dt.uint32
U16 = mybir.dt.uint16
U8 = mybir.dt.uint8
FP8X4 = mybir.dt.float8_e4m3fn_x4
MULT = mybir.AluOpType.mult
ADD = mybir.AluOpType.add
SIGMOID = mybir.ActivationFunctionType.Sigmoid
COPY = mybir.ActivationFunctionType.Copy

P = 128
PACK = 4
LINE = 4
GROUP = 16
K_PASS = P * PACK
PASSES = K // K_PASS
HALF = C // 2
SCALE_ROWS = 4
TURNS = 3
STAGING = 14
ROUNDED = 4
QUANTISED = 8

X_SCALAR_COLUMNS = 176
SCALAR_SHARE = 96
SCALAR_SHARE_LAST = (80, 80, 48, 48)


def tile_moe_tk_glu_sigmoid_kernel(tc, xT, w1, w3, w2, gate, offs, pos1, pos2, pos3, out):
    nc = tc.nc

    with ExitStack() as ctx:
        held = ctx.enter_context(tc.tile_pool(name="held", bufs=1))
        turns = ctx.enter_context(tc.tile_pool(name="turns", bufs=1))
        loads = ctx.enter_context(tc.tile_pool(name="loads", bufs=STAGING))
        work = ctx.enter_context(tc.tile_pool(name="work", bufs=ROUNDED))
        quant = ctx.enter_context(tc.tile_pool(name="quant", bufs=QUANTISED))
        small = ctx.enter_context(tc.tile_pool(name="small", bufs=E))
        psum_a = ctx.enter_context(tc.psum_pool(name="psum_a", bufs=2))
        psum_b = ctx.enter_context(tc.psum_pool(name="psum_b", bufs=2))
        psum_y = ctx.enter_context(tc.psum_pool(name="psum_y", bufs=4))

        def load_rows(rows):
            raw = loads.tile([P, PACK, rows.shape[1]], F32, name="raw", tag="raw", align_bytes=64)
            nc.sync.dma_start(out=raw[:], in_=rows.rearrange("(p j) w -> p j w", j=PACK))
            return raw

        def quantize(codes, scales, grouped):
            nc.vector.quantize_mx(out=codes.bitcast(FP8X4), scales=scales, in_=grouped)

        def interleave(copy, grouped, raw):
            copy(
                out=grouped.rearrange("p (c i) j -> p c j i", i=LINE),
                in_=raw.rearrange("p j (c i) -> p c j i", i=LINE),
            )

        def interleave_permuted(copy, grouped, raw, m0, m1):
            copy(
                out=grouped[:, :, m0:m1, :].rearrange("p t m (pair row) -> p m pair t row", row=2),
                in_=raw[:, :, PACK * m0 : PACK * m1].rearrange("p (pair row) (m t) -> p m pair t row", row=2, t=PACK),
            )

        warm = held.tile([P, 8], F32, name="warm")
        warm_out = held.tile([P, 8], F32, name="warm_out")
        nc.vector.memset(warm[:], 0.0)
        nc.scalar.activation(out=warm_out[:], in_=warm[:], func=SIGMOID)

        x_raw = [load_rows(xT[s * K_PASS : (s + 1) * K_PASS, :]) for s in range(PASSES)]
        slot_token = held.tile([P, E * C // GROUP], U16, name="slot_token")
        nc.sync.dma_start(slot_token[:], offs)

        x_codes = []
        x_scales = held.tile([P, T], U8, name="x_scales", align_bytes=64)
        nc.gpsimd.memset(x_scales[:], 0)
        for s in range(PASSES):
            codes = held.tile([P, T], U32, name="x_codes%d" % s, align_bytes=64)
            x_grouped = work.tile([P, T, PACK], BF16, name="x_grouped", tag="grouped", align_bytes=64)
            for copy, cols in ((nc.scalar.copy, slice(0, X_SCALAR_COLUMNS)), (nc.vector.tensor_copy, slice(X_SCALAR_COLUMNS, T))):
                interleave(copy, x_grouped[:, cols, :], x_raw[s][:, :, cols])
            quantize(codes[:], x_scales[SCALE_ROWS * s :, :], x_grouped[:].rearrange("p c j -> p (c j)"))
            x_codes.append(codes)

        identity = held.tile([P, P], F32, name="identity")
        make_identity(nc, identity[:])
        h_codes = held.tile([P, E * C], U32, name="h_codes", align_bytes=64)
        h_scales = held.tile([P, E * C], U8, name="h_scales", align_bytes=64)
        w2_codes = held.tile([P, E * N], U32, name="w2_codes", align_bytes=64)
        w2_scales = held.tile([P, E * N], U8, name="w2_scales", align_bytes=64)
        slot_codes, slot_scales = {}, {}

        def codes_turn(e):
            return "codes_turn%d" % (e % TURNS)

        def scales_turn(e):
            return "scales_turn%d" % (e % TURNS)

        def picks(e):
            return slot_token[:, e * C // GROUP : (e + 1) * C // GROUP]

        def gather_codes(e):
            slot_codes[e] = turns.tile([P, PASSES, C], U32, name="slot_codes", tag=codes_turn(e), align_bytes=64)
            for s in range(PASSES):
                nc.vector.tensor_copy(slot_codes[e][:, s, :], x_codes[s][:].indirect(picks(e)))

        def gather_scales(e):
            slot_scales[e] = turns.tile([P, C], U8, name="slot_scales", tag=scales_turn(e), align_bytes=64)
            nc.vector.tensor_copy(slot_scales[e][:], x_scales[:].indirect(picks(e)))

        def quantized_weights(w, e, s, share, pool, tag, pieces=1):
            raw = load_rows(w[e, s * K_PASS : (s + 1) * K_PASS, :])
            grouped = pool.tile([P, PACK, P, PACK], BF16, name="w_grouped", tag=tag, align_bytes=64)
            interleave_permuted(nc.scalar.copy, grouped, raw, 0, share)
            interleave_permuted(nc.vector.tensor_copy, grouped, raw, share, P)
            codes = quant.tile([P, H], U32, name="w_codes", align_bytes=64)
            scales = quant.tile([P, H], U8, name="w_scales", align_bytes=64)
            step = PACK // pieces
            for t in range(0, PACK, step):
                cols = slice(t * P, (t + step) * P)
                quantize(codes[:, cols], scales[:, cols], grouped[:, t : t + step, :, :].rearrange("p t m j -> p (t m j)"))
            return codes, scales, raw

        def first_layer_pass(banks, weights, e, s):
            codes, scales = weights[0], weights[1]
            for u in range(2):
                slots = slice(u * HALF, (u + 1) * HALF)
                for t in range(PACK):
                    cols = slice(t * P, (t + 1) * P)
                    nc.tensor.matmul_mx(
                        out=banks[u][:, t, :],
                        lhsT=codes[:, cols].bitcast(FP8X4),
                        lhsT_scale=scales[:, cols],
                        rhs=slot_codes[e][:, s, slots].bitcast(FP8X4),
                        rhs_scale=slot_scales[e][SCALE_ROWS * s :, slots],
                        start=(s == 0 and t == 0),
                        stop=(s == PASSES - 1 and t == PACK - 1),
                    )

        def sigmoid_over(bank, spent, column):
            sig = spent[:, :, column : column + HALF].rearrange("p g (c t) -> p g c t", t=PACK)
            nc.scalar.activation(out=sig, in_=bank[:].rearrange("p t (g c) -> p g c t", g=PACK), func=SIGMOID)
            return sig

        def hidden(bank, sig):
            h = work.tile([P, HALF, PACK], BF16, name="h", align_bytes=64)
            nc.vector.tensor_tensor(
                h[:].rearrange("p (g c) t -> p g c t", g=PACK), bank[:].rearrange("p t (g c) -> p g c t", g=PACK), sig, MULT
            )
            return h

        def quantize_hidden(h, e, u):
            slots = slice(e * C + u * HALF, e * C + (u + 1) * HALF)
            quantize(h_codes[:, slots], h_scales[:, slots], h[:].rearrange("p c t -> p (c t)"))

        def rounded_w2(e, copy, pool, tag):
            raw = pool.tile([P, PACK, N], F32, name="w2_raw", tag=tag, align_bytes=64)
            nc.sync.dma_start(out=raw[:], in_=w2[e].rearrange("(p j) n -> p j n", j=PACK))
            grouped = small.tile([P, N, PACK], BF16, name="w2_grouped", align_bytes=64)
            interleave(copy, grouped[:], raw[:])
            return grouped

        def quantize_w2(e):
            cols = slice(e * N, (e + 1) * N)
            quantize(w2_codes[:, cols], w2_scales[:, cols], w2_grouped[e][:].rearrange("p n j -> p (n j)"))

        def second_layer(experts, copy, pool, tag):
            acc = pool.tile([P, len(experts) * C], F32, name="y_acc", tag=tag)
            for place, e in enumerate(experts):
                cols = slice(e * N, (e + 1) * N)
                slots = slice(e * C, (e + 1) * C)
                nc.tensor.matmul_mx(
                    out=acc[:, place * C : (place + 1) * C],
                    lhsT=w2_codes[:, cols].bitcast(FP8X4),
                    lhsT_scale=w2_scales[:, cols],
                    rhs=h_codes[:, slots].bitcast(FP8X4),
                    rhs_scale=h_scales[:, slots],
                    start=True,
                    stop=True,
                )
            copy(out=y[:, experts[0] * C : (experts[-1] + 1) * C], in_=acc[:])

        last = E - 1
        gather_codes(0)
        gather_scales(0)
        gather_codes(1)
        for e in range(E):
            share = SCALAR_SHARE_LAST if e == last else (SCALAR_SHARE,) * (2 * PASSES)

            w1_q = [quantized_weights(w1, e, 0, share[0], turns, scales_turn(e + 1))]
            if e < last:
                gather_scales(e + 1)
            w1_q.append(quantized_weights(w1, e, 1, share[1], work, "grouped"))
            a = [psum_a.tile([P, PACK, HALF], F32, name="a", tag="a") for u in range(2)]
            for s in range(PASSES):
                first_layer_pass(a, w1_q[s], e, s)

            pool, tag = (turns, "result_turn") if e == last else (work, "grouped")
            w3_q = [quantized_weights(w3, e, 0, share[2], pool, tag)]
            w3_q.append(quantized_weights(w3, e, 1, share[3], turns, codes_turn(e + 2), 2 if e == last else 1))
            if e + 2 < E:
                gather_codes(e + 2)
            b = [psum_b.tile([P, PACK, HALF], F32, name="b", tag="b") for u in range(2)]
            for s in range(PASSES):
                first_layer_pass(b, w3_q[s], e, s)
            if e < last:
                sig = [sigmoid_over(a[0], w3_q[1][2], H - HALF), sigmoid_over(a[1], w3_q[1][2], 0)]
                h_pair = [hidden(b[u], sig[u]) for u in range(2)]
                for u in range(2):
                    quantize_hidden(h_pair[u], e, u)
            else:
                sig = [sigmoid_over(a[u], w3_q[u][2], 0) for u in range(2)]

        arrival = [last] + list(range(last))
        w2_grouped = {}
        for e in arrival:
            copy = nc.vector.tensor_copy if e in arrival[:2] else nc.scalar.copy
            pool, tag = (turns, "result_turn") if e == arrival[-1] else (loads, "raw")
            w2_grouped[e] = rounded_w2(e, copy, pool, tag)
        y = turns.tile([P, E * C], F32, name="y", tag="result_turn", align_bytes=64)

        quantize_w2(arrival[0])
        quantize_w2(arrival[1])
        h_last = [hidden(b[0], sig[0])]
        quantize_w2(arrival[2])
        h_last.append(hidden(b[1], sig[1]))
        for u in range(2):
            quantize_hidden(h_last[u], last, u)
            quantize_w2(arrival[3 + u])
        quantize_w2(arrival[-1])

        second_layer((0, 1), nc.scalar.copy, psum_y, "y_acc")
        second_layer((2,), nc.scalar.copy, psum_y, "y_acc")
        second_layer((3,), nc.scalar.copy, psum_y, "y_acc")
        second_layer((arrival[-1],), nc.vector.tensor_copy, psum_y, "y_acc")
        second_layer((last,), nc.vector.tensor_copy, psum_a, "a")

        gates = turns.tile([P, TOP, T], F32, name="gates", tag=codes_turn(last + 2), align_bytes=64)
        early, late = slice(0, T // 2), slice(T // 2, T)
        token_slot = []
        for r, pos in enumerate((pos1, pos2, pos3)):
            slot_list = held.tile([P, T // GROUP], U16, name="token_slot%d" % r)
            nc.sync.dma_start(slot_list[:], pos)
            token_slot.append(slot_list)
            nc.sync.dma_start(out=gates[:, r, early], in_=gate[r, :, early])
        nc.sync.dma_start(out=gates[:, :, late], in_=gate[:, :, late].rearrange("r p t -> p r t"))

        def results(r, tokens):
            return y[:].indirect(token_slot[r][:, tokens.start // GROUP : tokens.stop // GROUP])

        products = held.tile([P, TOP, T], F32, name="products")
        picked = held.tile([P, TOP, T // 2], F32, name="picked")
        partial = held.tile([P, T], F32, name="partial")
        total = held.tile([P, T], F32, name="total")
        early_blocks = [slice(t0, t0 + P) for t0 in range(early.start, early.stop, P)]
        late_blocks = [slice(t0, t0 + P) for t0 in range(late.start, late.stop, P)]

        for r in range(TOP):
            nc.scalar.activation(out=picked[:, r, :], in_=results(r, late), func=COPY)
        summed = [psum_y.tile([P, P], F32, name="summed", tag="y_acc") for block in early_blocks]
        for r in range(TOP):
            for tokens in early_blocks if r == TOP - 1 else [early]:
                nc.vector.tensor_tensor(products[:, r, tokens], results(r, tokens), gates[:, r, tokens], MULT)
            for place, block in enumerate(early_blocks):
                nc.tensor.matmul(
                    summed[place][:], products[:, r, block], identity[:], is_transpose=True, start=(r == 0), stop=(r == TOP - 1)
                )
        back = [psum_b.tile([P, P], F32, name="back", tag="b") for block in early_blocks]
        for place, block in enumerate(early_blocks):
            nc.scalar.copy(out=partial[:, block], in_=summed[place][:])
            nc.tensor.transpose(back[place][:], partial[:, block], identity[:])
        for place, block in enumerate(early_blocks):
            nc.scalar.copy(out=total[:, block], in_=back[place][:])
            nc.scalar.dma_start(out=out[:, block], in_=total[:, block])

        nc.vector.tensor_tensor(products[:, 0:2, late], picked[:, 0:2, :], gates[:, 0:2, late], MULT)
        nc.vector.tensor_tensor(products[:, 2, late], picked[:, 2, :], gates[:, 2, late], MULT)
        for block in late_blocks:
            nc.vector.tensor_tensor(partial[:, block], products[:, 0, block], products[:, 1, block], ADD)
        for block in late_blocks:
            nc.vector.tensor_tensor(total[:, block], partial[:, block], products[:, 2, block], ADD)
            nc.sync.dma_start(out=out[:, block], in_=total[:, block])
